import numpy as np, ml_dtypes
CORES = [35,38,43,46]
N = 4
BF = ml_dtypes.bfloat16
def gentries(a):
    return np.ascontiguousarray(a.reshape(8, 16, -1).transpose(0, 2, 1)).reshape(8, -1)
def gtable(e):
    e = np.asarray(e); return np.ascontiguousarray(e.reshape(8, -1, 16).transpose(0, 2, 1)).reshape(128, -1).astype(np.int32)
IT, M, CAP, ST, RO = 4096, 2048, 256, 3, 3
def forest(rng):
    k = np.full((N, 8, 2, M), M, np.int64); par = np.zeros((N, 8, M), np.int64); m = M // 8
    for q in range(N):
        for g in range(8):
            p = rng.permutation(M).reshape(8, m); par[q, g, p[1::2].reshape(-1)] = 1
            for l in range(7):
                u = rng.permutation(2 * m)[:m]; k[q, g, u // m, p[l, u % m]] = p[l + 1]
    return k, par
def labels(rng, e):
    lab = np.full((N, 8, IT), M, np.int64)
    for q in range(N):
        for g in range(8):
            n = int(e[q, g]); live = rng.permutation(M)[:n]; o = rng.permutation(IT)
            w = live[np.minimum((n * rng.random(IT - n) ** 2).astype(np.int64), n - 1)]
            lab[q, g, o[:n]] = live; lab[q, g, o[n:]] = np.where(rng.random(IT - n) < 0.06, M, w)
    return lab
def lot(rng, live):
    o = rng.permutation(IT); n = len(live); lab = np.full(IT, M, np.int64)
    lab[o[:n]] = live; lab[o[n:]] = np.where(rng.random(IT - n) < 0.06, M, live[rng.integers(0, n, IT - n)])
    return lab
def count(rng):
    return rng.integers(M * 5 // 8, M * 7 // 8, (N, 8))
def parts(rng, lab=None):
    if lab is None: lab = labels(rng, count(rng))
    k, par = forest(rng); n = np.zeros((N, 8, IT), np.int64); cur = np.zeros((N, 8, M), np.int64); siz = np.zeros((N, 8, M), np.int64)
    for q in range(N):
        for g in range(8):
            o = rng.permutation(IT); o = o[np.argsort(lab[q, g, o], kind="stable")]; s = lab[q, g, o]
            last = np.append(s[1:] != s[:-1], True)
            n[q, g, o] = np.where(last, o[np.searchsorted(s, s)], np.roll(o, -1))
            z = np.bincount(s, minlength=M + 1)[:M]; a = np.minimum(np.searchsorted(s, np.arange(M)), IT - 1)
            siz[q, g] = z; cur[q, g] = np.where(z > 0, o[a], rng.integers(0, IT, M))
    tgt = np.minimum(np.maximum(siz + rng.integers(-2, 4, siz.shape), 0), IT)
    return {"k": k, "par": par, "n": n, "cur": cur, "siz": siz, "tgt": tgt}
def values(rng):
    h = rng.choice(np.array([60, 90, 140, 230]), (N, 8, 1, 1))
    x = np.clip(rng.integers(40, 215, (N, 8, 1, IT)) + rng.integers(-40, 41, (N, 8, 16, IT)), 0, 254)
    key = np.clip((h * rng.random((N, 8, 1, M))).astype(np.int64) + rng.integers(-40, 41, (N, 8, 16, M)), 0, 254)
    return x, key
def pack(d, x, key):
    tab = lambda a: np.stack([gtable(b) for b in a])
    key = np.where(d["siz"][:, :, None, :] > 0, key, 255)
    return {"x": np.ascontiguousarray(x.reshape(N, 128, IT)).astype(np.float32).astype(BF), "ky": np.ascontiguousarray(key.reshape(N, 128, M)).astype(np.float32).astype(BF),
            "nxt": d["n"].astype(np.int32), "cur": tab(d["cur"]), "siz": tab(d["siz"]), "tgt": tab(d["tgt"]), "par": tab(d["par"]), "kl": tab(d["k"][:, :, 0]), "kr": tab(d["k"][:, :, 1])}
def setup_inputs(rng):
    d = parts(rng); x, key = values(rng)
    return pack(d, x, key)
def setup_inputs_room(rng):
    d = parts(rng); d["tgt"] = np.where(d["par"] == 0, 0, d["tgt"])
    x = rng.integers(40, 201, (N, 8, 16, IT)); key = rng.integers(0, 40, (N, 8, 16, M))
    for q in range(N):
        for g in range(8):
            live = rng.permutation(np.nonzero(d["siz"][q, g])[0]); e = len(live)
            n = int(rng.choice(np.array([0, 1, CAP - 1, CAP, CAP + 1, e])))
            if q == 0: n = (CAP, CAP + 1, e, CAP - 1, 1, 0, CAP, CAP + 1)[g]
            if q == 1: n = (CAP + 1, CAP, CAP, e, CAP, CAP, 0, 1)[g]
            key[q, g][:, live[:n]] = rng.integers(201, 255, (16, n))
    return pack(d, x, key)
def setup_inputs_ties(rng):
    d = parts(rng); c = np.array([0, 7, 8, 9, 16])
    place = np.argsort(rng.random((N, 8, 16, 1)), axis=2)
    a = rng.choice(c, (N, 8, 1, IT)); w = rng.integers(1, 100, (N, 8, 16, IT)) * (rng.random((N, 8, 1, IT)) < 0.8)
    x = np.where(place < a, 100 - w, 100 + w)
    key = 100 + (place < rng.choice(c, (N, 8, 1, M))).astype(np.int64); key[:, ::2] = 100
    return pack(d, x, key)
def setup_inputs_ends(rng):
    e = count(rng); e[:, 2] = M; e[:, 3] = M // 16; lab = labels(rng, e)
    for q in range(N):
        n = int(e[q, 0]); lab[q, 0] = M; lab[q, 0, rng.permutation(IT)[:n]] = rng.permutation(M)[:n]
        live = rng.permutation(M)[:M // 4]; lab[q, 1] = live[0]; lab[q, 1, rng.permutation(IT)[:M // 4]] = live
    d = parts(rng, lab); d["k"][:, 4, 0] = M; d["k"][:, 5, 1] = M; h = M // 2
    for q in range(N):
        a = rng.permutation(M); d["k"][q, 7] = M; d["k"][q, 7, 0, a[:h]] = a[h:]; d["k"][q, 7, 1, a[h:]] = a[:h]
        d["par"][q, 7, a[:h]] = 0; d["par"][q, 7, a[h:]] = 1
        for g, b in ((4, 0), (5, 1)):
            k = d["k"][q, g]; lone = np.all(k == M, axis=0); lone[k[k < M]] = False; d["par"][q, g, lone] = b
    z = d["siz"]; u = rng.integers(0, 4, z.shape); big = np.argmax(z[:, 1], axis=1); r = np.arange(N)
    for q in range(N):
        w = np.nonzero((z[q, 1] > 0) & (d["par"][q, 1] != d["par"][q, 1, big[q]]))[0]
        if len(w) > 0:
            w = int(rng.choice(w)); k = d["k"][q, 1]; k[(k == big[q]) | (k == w)] = M
            k[0, big[q]] = w; k[1, big[q]] = M
    d["tgt"] = np.where(u == 0, 0, np.where(u == 1, z, np.where(u == 2, np.minimum(z + 1, IT), IT)))
    d["tgt"][r, 1, big] = z[r, 1, big] + 1 - r % 2
    x, key = values(rng)
    return pack(d, x, key)
def setup_inputs_full(rng):
    h = M // 2; m = M // 4; lab = labels(rng, count(rng)); a = np.argsort(rng.random((N, 8, M)), axis=2); top = np.zeros((N, 5), np.int64)
    for q in range(N):
        for g, w in ((0, a[q, 0]), (1, a[q, 1, h:]), (2, a[q, 2]), (3, a[q, 3]), (4, np.concatenate([a[q, 4, :m // 2], a[q, 4, m:2 * m], a[q, 4, 3 * m:]]))):
            lab[q, g] = lot(rng, w)
        lab[q, 5] = a[q, 5, 1]; lab[q, 5, rng.permutation(IT)[:(IT - 1, IT, IT - 1, IT - 2)[q % 4]]] = a[q, 5, 0]
        lab[q, 6] = a[q, 6, 15:][rng.integers(0, M - 15, IT)]; o = rng.permutation(IT); at = 0
        for f in range(5):
            kid = int(rng.integers(1, 41)); s = IT // 8 + 45 + 4 * int(rng.integers(0, 14)) + 2 * (f % 2); top[q, f] = s + f % 2
            for v, n in ((f, s - kid), (5 + f, kid), (10 + f, kid)):
                lab[q, 6, o[at:at + n]] = a[q, 6, v]; at += n
    d = parts(rng, lab); k, par, t, z = d["k"], d["par"], d["tgt"], d["siz"]; k[:, :7] = M
    x, key = values(rng)
    for g in (0, 1, 2, 4): t[:, g] = np.minimum(z[:, g] + rng.integers(1, 50, (N, M)), IT)
    x[:, 3] = rng.integers(40, 201, (N, 16, IT)); key[:, 3] = rng.integers(0, 40, (N, 16, M))
    x[:, 4] = np.where(rng.random((N, 1, IT)) < 0.3, 254, rng.integers(200, 255, (N, 16, IT)))
    for q in range(N):
        for g in (0, 1):
            b = (q + g) % 2; k[q, g, rng.integers(0, 2, h), a[q, g, :h]] = a[q, g, h:]
            par[q, g, a[q, g, :h]] = b; par[q, g, a[q, g, h:]] = 1 - b
        w = rng.permutation(M - 16)[:16]; k[q, 2, rng.integers(0, 2, 16), np.arange(M - 16, M)] = w
        par[q, 2] = q % 2; par[q, 2, w] = 1 - q % 2
        key[q, 3][:, int(rng.integers(0, 16))::16] = rng.integers(201, 255, (16, M // 16))
        p = a[q, 4]; b = (q // 2) % 2; k[q, 4, 1, p[:m]] = p[m:2 * m]; k[q, 4, 0, p[:m:2]] = p[2 * m:3 * m:2]
        par[q, 4, p[:m]] = b; par[q, 4, p[m:3 * m]] = 1 - b
        c = np.where(rng.random(m) < 0.5, 16, rng.integers(9, 17, m)); place = np.argsort(rng.random((16, m)), axis=0)
        key[q, 4][:, p[m:2 * m]] = np.where(place < c, 254, rng.integers(100, 255, (16, m)))
        key[q, 4][:, p[3 * m:3 * m + m // 2]] = 254
        b = int(rng.integers(0, 2)); u, w = int(a[q, 5, 0]), int(a[q, 5, 1]); k[q, 5, int(rng.integers(0, 2)), u] = w
        par[q, 5, u] = b; par[q, 5, w] = 1 - b; t[q, 5, u] = (IT, IT, IT - 1, IT - 1)[q % 4]
        p = a[q, 6]; k[q, 6, 0, p[:5]] = p[5:10]; k[q, 6, 1, p[:5]] = p[10:15]
        par[q, 6, p[:5]] = 0; par[q, 6, p[5:15]] = 1; t[q, 6, p[:5]] = top[q]
    return pack(d, x, key)
def setup_inputs_spread(rng):
    d = parts(rng)
    d["tgt"] = np.minimum(np.exp2(13 * rng.random((N, 8, M))).astype(np.int64) - 1, IT)
    x = np.minimum((np.exp2(8 * rng.random((N, 8, 1, IT))) * rng.random((N, 8, 16, IT))).astype(np.int64), 254)
    key = np.minimum((np.exp2(8 * rng.random((N, 8, 1, M))) * rng.random((N, 8, 16, M))).astype(np.int64), 254)
    return pack(d, x, key)
def check_inputs(d):
    bad = []
    for k, hi in (("x", 254), ("ky", 255)):
        a = np.asarray(d[k]).astype(np.float32)
        if not np.all((a >= 0) & (a <= hi) & (a == np.floor(a))): bad.append("whole numbers and range of " + k)
    for k, hi in (("nxt", IT - 1), ("cur", IT - 1), ("siz", IT), ("tgt", IT), ("par", 1), ("kl", M), ("kr", M)):
        if np.min(d[k]) < 0 or np.max(d[k]) > hi: bad.append("range of " + k)
    if bad: return bad
    n = np.asarray(d["nxt"]).astype(np.int64)
    if np.any(np.sort(n, axis=2) != np.arange(IT)): return ["every item once in a row of nxt"]
    cur, siz, par, kl, kr = [np.stack([gentries(a) for a in d[k]]).astype(np.int64) for k in ("cur", "siz", "par", "kl", "kr")]
    live = siz > 0; key = np.asarray(d["ky"]).astype(np.float32).reshape(N, 8, 16, M)
    if np.any(np.where(live[:, :, None, :], key > 254, key != 255)): bad.append("keys of empty and of other nodes")
    lab = np.tile(np.arange(IT), (N, 8, 1)); j = n
    for i in range((IT - 1).bit_length()):
        lab = np.minimum(lab, np.take_along_axis(lab, j, 2)); j = np.take_along_axis(j, j, 2)
    def tally(a, w, k):
        a = (a + np.arange(N * 8).reshape(N, 8, 1) * k)[w]
        return np.bincount(a, minlength=N * 8 * k).reshape(N, 8, k)
    c = tally(lab, np.ones(lab.shape, bool), IT); own = np.take_along_axis(lab, cur, 2)
    if np.any(live & (np.take_along_axis(c, own, 2) != siz)): bad.append("sizes are the rings' numbers of items")
    if np.max(tally(own, live, IT)) > 1: bad.append("nodes that aren't empty have different rings")
    kids = np.concatenate([kl, kr], axis=2)
    if np.max(tally(kids, kids < M, M)) > 1: bad.append("a node stands at most once in kl and kr")
    px = np.concatenate([par, np.full((N, 8, 1), 2, np.int64)], axis=2)
    if np.any(np.take_along_axis(px, kids, 2) == np.concatenate([par, par], axis=2)): bad.append("parities of kids")
    return bad
def reference(x, ky, nxt, cur, siz, tgt, par, kl, kr):
    X = x.astype(np.float32).reshape(N, 8, 16, IT)
    K = np.concatenate([ky.astype(np.float32).reshape(N, 8, 16, M), np.full((N, 8, 16, 1), 255, np.float32)], axis=3)
    nx = nxt.astype(np.int64)
    C, Z, T, P, A, B = [np.stack([gentries(a) for a in b]).astype(np.int64) for b in (cur, siz, tgt, par, kl, kr)]
    none = np.zeros((N, 8, 1), np.int64); C = np.concatenate([C, none], axis=2); Z = np.concatenate([Z, none], axis=2)
    for t in range(RO):
        le = np.take_along_axis(K, A[:, :, None, :], 3) <= np.take_along_axis(K, B[:, :, None, :], 3)
        ch = np.where(np.add.reduce(le, axis=2, dtype=np.int64) >= 9, A, B)
        go = (P == t % 2) & (Z[..., :M] < T) & (np.take_along_axis(Z, ch, 2) > 0)
        i, j, v = np.nonzero(go & (Z[..., :M] > 0)); c = ch[i, j, v]
        a, b = C[i, j, v], C[i, j, c]; na, nb = nx[i, j, a], nx[i, j, b]
        nx[i, j, a] = nb; nx[i, j, b] = na
        i, j, v = np.nonzero(go); c = ch[i, j, v]
        C[i, j, v] = np.where(Z[i, j, v] > 0, C[i, j, v], C[i, j, c])
        K[i, j, :, v] = K[i, j, :, c]; K[i, j, :, c] = 255
        Z[i, j, v] = Z[i, j, v] + Z[i, j, c]; Z[i, j, c] = 0
        live = Z[..., :M] > 0; s = C[..., :M]; lv = np.full((N, 8, M), -1, np.int64)
        for k in range(ST):
            s = np.take_along_axis(nx, s, 2)
            low = np.take_along_axis(X, s[:, :, None, :], 3) < K[..., :M]
            lv = np.where((lv < 0) & live & (np.add.reduce(low, axis=2, dtype=np.int64) >= 9), s, lv)
        C[..., :M] = np.where(live, s, C[..., :M])
        has = (lv >= 0).astype(np.int64); pl = np.add.accumulate(has, axis=2) - 1
        i, j, v = np.nonzero((has == 1) & (pl < CAP))
        e = np.full((N, 8, CAP), -1, np.int64); e[i, j, pl[i, j, v]] = lv[i, j, v]
        come = np.roll(np.take_along_axis(X, np.maximum(e, 0)[:, :, None, :], 3), 1, axis=0)
        i, j, k = np.nonzero((e >= 0) & (np.roll(e, 1, axis=0) >= 0))
        X[i, j, :, e[i, j, k]] = come[i, j, :, k]
    return {"yx": X.reshape(N, 128, IT).astype(BF), "yk": np.ascontiguousarray(K[..., :M]).reshape(N, 128, M).astype(BF), "yn": nx.astype(np.float32),
            "yc": np.stack([gtable(a) for a in np.ascontiguousarray(C[..., :M])]).astype(np.float32)}

@@ -1,0 +1,607 @@
+import numpy as np
+from concourse.mybir import AluOpType, AxisListType, ActivationFunctionType
+
+A = AluOpType
+AF = ActivationFunctionType
+IT, M, RO = 4096, 2048, 3
+SENT = IT + M
+KW, NW = M + 16, SENT + 16
+
+SCRATCH = {"KK": 4 * KW, "XX": NW, "NN": NW, "GL": M, "LE": M, "LT": 3 * M, "PP": M, "ZR": M, "SR": 9 * M, "SB": M,
+           "W0": 2 * M, "JK": M, "SD": 3 * 272, "RV0": 272, "RV1": 272, "RV2": 272, "BB": 80 * 128}
+SCRATCH = {k: ("sbuf", [128, n], "bfloat16") for k, n in SCRATCH.items()}
+SCRATCH.update({k: ("sbuf", [128, n], "float32") for k, n in (("SF", M), ("W1", 2 * M), ("W2", 2 * M), ("FF", 36 * 128))})
+SCRATCH.update({"II": ("sbuf", [128, 20 * 128], "int32"), "UU": ("sbuf", [128, 30 * 128], "uint16")})
+SCRATCH.update({"PS%d" % k: ("psum", [128, 512], "float32") for k in range(8)})
+SEMAPHORES = ["cV", "cS", "cP", "cG"] + ["d%d" % k for k in range(40)] + ["rv0", "rv1", "rv2", "sn0", "sn1", "sn2"]
+
+WENG = ("V", "S", "S")
+XS = ((), (), ())
+NVS = (0, 0, 5)
+DCH = (64, 128, 128)
+NMS = 2560
+GCH, SCH = 1024, 512
+CY, GA, SC, PEC, LAT = 1.04e-3, 1.56, 3.8, 0.6e-3, 0.12
+SEED, TRIES, TEMP = 13, 11000, 0.45
+SIZE = {"float32": 4, "int32": 4, "bfloat16": 2, "uint16": 2}
+
+
+def plan(T, g, peer):
+    ops, bank, npv = [], {}, [0]
+    top = {"FF": 0, "BB": 0, "II": 0, "UU": 0}
+
+    def new(b, n=128):
+        lo = top[b]
+        top[b] = lo + (n + 15) // 16 * 16
+        assert top[b] <= SCRATCH[b][1][1], b
+        return (b, lo, lo + n, None)
+
+    def reg(b, lo, n):
+        return (b, lo, lo + n, None)
+
+    def sub(r, lo, n, tag=None):
+        return (r[0], r[1] + lo, r[1] + lo + n, tag)
+
+    def psum(n=128):
+        npv[0] += 1
+        return (("ps", npv[0]), 0, n, None)
+
+    def isps(r):
+        return isinstance(r[0], tuple)
+
+    def ap(r):
+        return T["PS%d" % bank[r[0]] if isps(r) else r[0]][:, r[1]:r[2]]
+
+    def rows(r, first, step):
+        return T[r[0]][first::step, r[1]:r[2]]
+
+    def val(s):
+        return ap(s) if isinstance(s, tuple) else s
+
+    def op(eng, dur, rd, wr, fn, name, lat=LAT, inc=1, kind="c"):
+        ops.append({"eng": eng, "dur": dur, "rd": rd, "wr": wr, "fn": fn, "lat": lat, "inc": inc, "kind": kind, "name": name})
+
+    def vc(n, f):
+        return 0.05 + max(64, n * f) * CY
+
+    def half(*rs):
+        return 0.5 if all(not isps(r) and SIZE[SCRATCH[r[0]][2]] == 2 for r in rs) else 1.0
+
+    def ts(o, i, s1, s2, o0, o1=None):
+        rd = [i] + [s for s in (s1, s2) if isinstance(s, tuple)]
+        if o1 is None:
+            f = lambda: g.vector.tensor_scalar(ap(o), ap(i), val(s1), None, o0)
+        else:
+            f = lambda: g.vector.tensor_scalar(ap(o), ap(i), val(s1), val(s2), o0, o1)
+        op("V", vc(i[2] - i[1], half(o, i)), rd, [o], f, "ts")
+        return o
+
+    def tt(o, a, b, o0):
+        f = half(o, a, b) * (1 if isps(a) or isps(b) else 2)
+        op("V", vc(a[2] - a[1], f), [a, b], [o], lambda: g.vector.tensor_tensor(ap(o), ap(a), ap(b), o0), "tt")
+        return o
+
+    def cp(o, i):
+        op("V", vc(i[2] - i[1], half(o, i)), [i], [o], lambda: g.vector.tensor_copy(ap(o), ap(i)), "cp")
+        return o
+
+    def ms(o, c):
+        op("V", vc(o[2] - o[1], half(o)), [], [o], lambda: g.vector.memset(ap(o), float(c)), "ms")
+        return o
+
+    def act(o, i, fn=AF.Identity, bias=0.0, scale=1.0, acc=None):
+        rd = [i] + [s for s in (bias, scale) if isinstance(s, tuple)]
+        if acc is None:
+            f = lambda: g.scalar.activation(ap(o), ap(i), fn, bias=val(bias), scale=val(scale))
+        else:
+            f = lambda: g.scalar.activation(ap(o), ap(i), fn, bias=val(bias), scale=val(scale), accum_out=ap(acc))
+        op("S", 0.07 + max(64, i[2] - i[1]) * CY, rd, [o] + ([acc] if acc else []), f, "act")
+        return o
+
+    def iota(o, pat, base, cm):
+        if o[0] != "II":
+            f = lambda: g.iota(ap(o), pat, base, cm, allow_small_or_imprecise_dtypes=True)
+        else:
+            f = lambda: g.iota(ap(o), pat, base, cm)
+        op("G", 0.13 + 2 * (o[2] - o[1]) * CY, [], [o], f, "iota")
+        return o
+
+    def fill(o, c):
+        return iota(o, [[0, o[2] - o[1]]], c, 0)
+
+    def chunks(n, c):
+        return [(lo, min(c, n - lo)) for lo in range(0, n, c)]
+
+    def sgather(o, win, off):
+        for lo, n in chunks(o[2] - o[1], GCH):
+            oo, ff = sub(o, lo, n), sub(off, lo // 16, n // 16)
+            op("S", 0.065 + n * GA * CY, [win, ff], [oo],
+               lambda oo=oo, ff=ff: g.scalar.activation(ap(oo), ap(win).indirect(ap(ff)), AF.Copy), "sg")
+            ops[-1]["alt"] = lambda oo=oo, ff=ff: g.vector.tensor_copy(ap(oo), ap(win).indirect(ap(ff)))
+
+    def vgather(o, win, off, in1, o0):
+        for lo, n in chunks(o[2] - o[1], GCH):
+            oo, ff, i1 = sub(o, lo, n), sub(off, lo // 16, n // 16), sub(in1, lo, n)
+            op("V", 0.05 + n * GA * CY, [win, ff, i1], [oo],
+               lambda oo=oo, ff=ff, i1=i1: g.vector.tensor_tensor(ap(oo), ap(win).indirect(ap(ff)), ap(i1), o0), "vg")
+
+    def scatter(eng, win, off, src):
+        for lo, n in chunks(src[2] - src[1], SCH):
+            ss, ff = sub(src, lo, n), sub(off, lo // 16, n // 16)
+            f = fv = lambda ss=ss, ff=ff: g.vector.tensor_copy(ap(win).indirect(ap(ff)), ap(ss))
+            if eng == "S":
+                f = lambda ss=ss, ff=ff: g.scalar.activation(ap(win).indirect(ap(ff)), ap(ss), AF.Silu)
+            op(eng, 0.06 + n * SC * CY, [ss, ff], [win], f, "sc")
+            if eng == "S":
+                ops[-1]["alt"] = fv
+
+    def mm(o, terms):
+        rd, cnt = [], 0
+        for l, r, st in terms:
+            rd += [l, r]
+            cnt += 16 if st else 1
+
+        def f():
+            pairs = []
+            for l, r, st in terms:
+                if st:
+                    pairs += [(T[l[0]][:, l[1] + 16 - i:l[1] + 144 - i], T[r[0]][:, r[1] + i:r[2]:16]) for i in range(16)]
+                else:
+                    pairs.append((ap(l), ap(r)))
+            return [g.tensor.matmul(ap(o), l, r, k == 0, k == cnt - 1) for k, (l, r) in enumerate(pairs)][-1]
+        op("P", 0.06 + cnt * max(64, o[2] - o[1]) * PEC, rd, [o], f, "mm")
+        return o
+
+    def tolist(o, terms, extra=()):
+        for lo, n in chunks(terms[0][1][2] - terms[0][1][1], GCH):
+            mm(sub(o, lo // 16, n // 16), [(s, sub(tab, lo, n), True) for s, tab in terms]
+               + [(l, sub(r, lo // 16, n // 16), False) for l, r in extra])
+        return o
+
+    def dma(q, rd, wr, pairs, nbytes, nrows=128, **kw):
+        e = {"Y": g.sync, "S": g.scalar, "G": g}[q]
+        op(q, {"Y": 0.1, "S": 0.1, "G": 1.0}[q] * len(pairs), rd, wr, lambda: [e.dma_start(o(), i(), **kw) for o, i in pairs],
+           "dma", lat=2.0 + nbytes / 250e3 + nrows * 0.004, inc=16 * len(pairs), kind="d")
+
+    def load(q, name, r, nbytes=65536):
+        dma(q, [], [r], [(lambda: ap(r), lambda: T[name][:])], nbytes)
+        return r
+
+    def torow(q, tab, row, lst):
+        dma(q, [lst], [sub(tab, 0, tab[2] - tab[1], "r%d" % row)], [(lambda: rows(tab, row, 16), lambda: ap(lst))], 65536)
+
+    K = [reg("KK", t * KW, M) for t in range(4)]
+    KWIN = [reg("KK", t * KW, KW) for t in range(4)]
+    kl = load("Y", "kl", new("II"))
+    kr = load("S", "kr", new("II"))
+    load("Y", "ky", K[0], 524288)
+    nx = load("S", "nxt", new("II", 256), 131072)
+    cur, siz, tgt, par = [load("Y", n, new("II")) for n in ("cur", "siz", "tgt", "par")]
+    SB, SF = reg("SB", 0, M), reg("SF", 0, M)
+    load("Y", "ky", SB, 1048576)
+    load("Y", "x", reg("XX", 0, IT), 2097152)
+    XW, NWIN, NLO = reg("XX", 0, NW), reg("NN", 0, NW), reg("NN", 0, IT)
+
+    X1 = iota(new("FF", 256), [[1, 256]], 1, 0)
+    pi = iota(new("II", 1), [[0, 1]], 0, 1)
+    pf = iota(new("FF", 1), [[0, 1]], 0, 1)
+    p1 = iota(new("FF", 1), [[0, 1]], 1, 1)
+    vp = iota(new("FF"), [[16, 128]], 0, 1)
+    dh = iota(new("BB"), [[0, 128]], 128 * 128, 128)
+    dh0 = iota(new("BB"), [[0, 128]], 96 * 128, 128)
+    dl = iota(new("BB"), [[1, 128]], 128, 0)
+    ai = ts(new("II", 1), pi, 15, None, A.bitwise_and)
+    a7 = ts(new("II", 1), pi, 7, None, A.bitwise_and)
+    g16 = tt(new("FF", 1), pf, ai, A.subtract)
+    g17 = ts(new("FF", 1), g16, 17.0, None, A.add)
+    x144, x128 = sub(X1, 0, 144), sub(X1, 0, 128)
+    ALL = ts(new("BB", 144), x144, g17, None, A.is_equal)
+    m4 = ts(new("FF", 1), ai, 4.0, 8192.0, A.is_equal, A.mult)
+    m08 = ts(new("FF", 1), a7, 0.0, None, A.is_equal)
+    m2 = ts(new("FF", 1), ai, 2.0, 16.0, A.is_equal, A.mult)
+    m082 = tt(new("FF", 1), m2, m08, A.add)
+    m412 = ts(new("FF", 1), a7, 4.0, None, A.is_equal)
+    AP8, AN8, R4, R08, R2, R082, R412 = [act(new("BB", 144), ALL, scale=s) for s in (8192.0, -8192.0, m4, m08, m2, m082, m412)]
+    I1 = ts(new("BB"), x128, p1, None, A.is_equal)
+    I2, I8, IB, IQ, IZ, IG = [act(new("BB"), I1, scale=s) for s in (2.0, 8.0, -262144.0, -4096.0, 4096.0, -524288.0)]
+    b1 = ts(new("BB"), x128, g16, None, A.is_gt)
+    b2 = ts(new("BB"), x128, g17, None, A.is_lt)
+    BD = tt(new("BB"), b1, b2, A.mult)
+    b3 = ts(b2, x128, pf, -1.0, A.is_le, A.mult)
+    NUP = tt(new("BB"), b1, b3, A.mult)
+    cq = ts(new("FF", 1), g16, -128.0, -16512.0, A.mult, A.add)
+    CQ = act(new("BB"), x128, bias=cq, scale=0.0)
+    C2, C17, CM1 = fill(new("BB"), 2), fill(new("BB"), 17), fill(new("BB"), -1)
+    if any(XS):
+        AH = act(new("BB", 144), ALL, scale=0.5)
+        IN1, IN8 = act(new("BB"), I1, scale=-1.0), act(new("BB"), I1, scale=-8.0)
+    vm = ts(new("FF"), vp, g16, -float(M), A.subtract, A.add)
+    tN = act(new("FF"), vm, bias=float(IT + M))
+    kb = act(new("FF", 16), sub(vm, 0, 16), bias=0.5 + M)
+    tX = sub(tN, 0, 16)
+    RA = act(new("BB", 144), ALL, scale=cp(new("FF", 1), ai))
+    for t in range(3):
+        fill(reg("KK", t * KW + M, 16), 255)
+    for lo in range(0, IT, 512):
+        (ms if lo < NMS else fill)(reg("NN", lo, 512), 0)
+    for lo, n in chunks(NW - IT, 256):
+        act(reg("NN", IT + lo, n), sub(X1, 0, n), bias=SENT / 2.0, scale=0.0)
+    W = [reg("W%d" % t, 0, 2 * M) for t in range(3)]
+    WU = [reg("W%d" % t, M, M) for t in range(3)]
+    for lo in range(0, M, 512):
+        fill(sub(WU[0], lo, 512), 0)
+    for t in range(3):
+        torow("G" if t else "Y", WU[t], 0, dh0)
+        torow("G" if t else "Y", WU[t], 8, dl)
+    torow("Y", SB, 0, dh)
+    torow("Y", SB, 8, dl)
+    dma("G", [SB], [SF], [(lambda: ap(SF), lambda: ap(SB))], 1048576)
+    for lo, n in chunks(NW - IT, 512):
+        fill(reg("XX", IT + lo, n), 255)
+    T1, T2 = new("FF", 144), new("BB", 144)
+    fill(sub(T1, 128, 16), 0)
+
+    nh = cp(new("BB", 256), nx)
+    nl = tt(new("BB", 256), nx, nh, A.subtract)
+    torow("Y", NLO, 0, nh)
+    torow("Y", NLO, 8, nl)
+    zh = cp(new("BB"), siz)
+    zl = tt(new("BB"), siz, zh, A.subtract)
+    zp = psum(256)
+    mm(sub(zp, 0, 128), [(zh, I1, False)])
+    mm(sub(zp, 128, 128), [(zl, I1, False)])
+    zt = act(new("BB", 256), zp, AF.Copy)
+    ZR = reg("ZR", 0, M)
+    dma("Y", [zt], [ZR], [(lambda k=k: T.ZR[16 * (k % 8) + 4 + 8 * (k // 8):16 * (k % 8) + 5 + 8 * (k // 8), :],
+                           lambda k=k: ap(sub(zt, 16 * k, 16))) for k in range(16)], 65536, nrows=2048)
+
+    klu, kru = cp(new("UU"), kl), cp(new("UU"), kr)
+    T1p = tt(new("FF"), tgt, par, A.mult)
+    T0p = tt(new("FF"), tgt, T1p, A.subtract)
+    room = tt(new("FF"), T0p, siz, A.subtract)
+    nwl = [ts(new("BB"), room, 0.5, None, A.is_lt), tt(new("BB"), siz, T1p, A.is_ge), None]
+    nwd = [None, act(new("BB"), T1p, AF.Relu, bias=1.0, scale=-1.0), act(new("BB"), T0p, AF.Relu, bias=1.0, scale=-1.0)]
+    c0 = ts(new("FF"), siz, 0.5, float(SENT), A.is_lt, A.mult)
+    Cf = tt(c0, c0, cur, A.max)
+    Cu = cp(new("UU"), Cf)
+    Cn = ts(new("FF"), cur, 8192.0, None, A.add)
+    PPr, GL, LE = reg("PP", 0, M), reg("GL", 0, M), reg("LE", 0, M)
+    has, hs, sig, cb = new("BB"), new("BB"), new("BB", 384), new("BB")
+    G1, G2, ER = new("BB", 256), new("BB", 256), new("BB", 256)
+    acc, e3, em, c16 = new("FF", 16), new("FF", 16), new("FF", 16), new("BB", 16)
+    T3 = new("BB", 144)
+    fill(sub(T3, 128, 16), 0)
+    kept = gone = S3p = None
+
+    for t in range(RO):
+        pen = [nwl[0]] if t == 0 else [nwd[t], tt(new("BB"), nwl[t], kept, A.min)]
+        sgather(GL, KWIN[t], klu)
+        vgather(LE, KWIN[t], kru, GL, A.is_ge)
+        emp = act(new("BB"), tolist(psum(), [(R4, GL)]), AF.Relu, bias=-254.0, scale=1.0 / 8192.0)
+        a2, cr, owu = new("FF"), new("FF"), new("UU")
+        for lo, n in chunks(128, DCH[t]):
+            le = sub(LE, 16 * lo, 16 * n)
+            pl = tolist(psum(n), [(AP8, le)], [(IQ, C17)] + [(IB, sub(x, lo, n)) for x in pen + [emp]])
+            pr = tolist(psum(n), [(AN8, le)], [(IZ, C17)] + [(IB, sub(x, lo, n)) for x in pen])
+            a, c = sub(a2, lo, n), sub(cr, lo, n)
+            tt(a, pl, sub(kl, lo, n), A.min)
+            tt(c, pr, sub(kr, lo, n), A.min)
+            tt(a, a, sub(vm, lo, n), A.max)
+            tt(a, a, c, A.max)
+            ts(sub(owu, lo, n), a, float(M), None, A.add)
+        gs = act(new("BB"), a2, AF.Sign, bias=0.5)
+        if t > 0:
+            pg = mm(psum(), [(I8, gone, False), (IG, gs, False), (IB, C2, False)])
+        if t < 2:
+            base = ts(new("II"), a2, float(M), None, A.add)
+            ts(base, base, M - 1, None, A.bitwise_and)
+            if t > 0:
+                tt(base, pg, base, A.max)
+            sgather(K[t + 1], KWIN[t], ts(new("UU"), base, float(M), None, A.min))
+        if t == 0:
+            scatter("V", W[0], owu, SB)
+        else:
+            scatter(WENG[t], W[t], owu, SF)
+            dma("G", [W[t]], [WU[0]], [(lambda: rows(WU[0], 0, 8), lambda t=t: rows(WU[t], 0, 8))], 65536, nrows=16)
+        pq = tolist(psum(), [(R08, WU[0])], [(I1, CQ), (IQ, gs)])
+        xi = tt(new("II"), pq, a2, A.max)
+        gone = act(new("BB"), pq, AF.Relu, bias=-3000.0)
+        if t < 2:
+            kept = act(new("BB"), pq, AF.Relu, bias=3000.0, scale=-1.0)
+        tks = act(new("BB"), pq, AF.Sign, bias=-3000.0)
+        if t == 2:
+            sgather(K[t + 1], KWIN[t], ts(new("UU"), tt(new("FF"), pg, xi, A.max), float(M), None, A.min))
+        ptu = cp(new("UU"), ts(new("II"), xi, M - 1, None, A.bitwise_and))
+        Q, S2, S3 = [reg("SR", (3 * t + k) * M, M) for k in range(3)]
+        sgather(PPr, NWIN, Cu)
+        if t == 0:
+            dma("Y", [ZR], [PPr], [(lambda: rows(PPr, 4, 8), lambda: rows(ZR, 4, 8))], 65536, nrows=16)
+        sgather(Q, PPr, ptu)
+        pk = tolist(psum(), [(R2, Q)] + ([(R082, S3p)] if t else []), [(IQ, tks), (IQ, gs)])
+        du = cp(new("UU"), tt(new("FF"), pk if t else tt(new("FF"), pk, Cf, A.max), tN, A.min))
+        S3p = S3
+        su = [new("UU") for _ in range(3)]
+        for lo, n in chunks(M, GCH):
+            p = mm(psum(n // 16), [(R08, sub(Q, lo, n), True), (I8, sub(gone, lo // 16, n // 16), False)])
+            ts(sub(su[0], lo // 16, n // 16), p, float(SENT), None, A.min)
+        if t == 0:
+            gz = act(new("FF"), tolist(psum(), [(R412, Q)], [(IZ, gs), (IZ, CM1)]), AF.Relu)
+            nwl[2] = tt(new("BB"), gz, room, A.is_ge)
+        scatter("V", NWIN, du, Q)
+        Cf = new("FF")
+        for k, tab in ((1, S2), (2, S3)):
+            sgather(tab, NWIN, su[k - 1])
+            for lo, n in chunks(M, GCH):
+                p = mm(psum(n // 16), [(R08 if k == 1 else R082, sub(tab, lo, n), True)])
+                ts(sub(su[k], lo // 16, n // 16), p, float(SENT), None, A.min)
+                if k == 2:
+                    act(sub(Cf, lo // 16, n // 16), p, AF.Copy)
+        Cu = su[2]
+        if t < 2:
+            Cn = act(Cn, tt(Cn, Cn, Cf, A.min), bias=8192.0)
+        else:
+            ci = tt(new("II"), Cn, Cf, A.min)
+            Cn = cp(Cn, ts(ci, ci, 8191, None, A.bitwise_and))
+        for k in range(3):
+            pc = psum()
+            for h in range(2):
+                l, u, o = reg("LT", k * M + 1024 * h, 1024), sub(su[k], 64 * h, 64), sub(pc, 64 * h, 64)
+                ex = [(I8, sub(sig, 128 * j + 64 * h, 64), False) for j in range(2 if k == 2 else 0)]
+                if 2 * k + h in XS[t]:
+                    sgather(l, XW, u)
+                    for j in (0, 512):
+                        d = mm(psum(512), [(I1, sub(l, j, 512), False), (IN1, sub(K[t + 1], 1024 * h + j, 512), False)])
+                        act(sub(l, j, 512), d, AF.Sign, bias=-0.5, scale=-1.0)
+                    mm(o, [(AH, l, True), (IN8, sub(CM1, 0, 64), False)] + ex)
+                else:
+                    vgather(l, XW, u, sub(K[t + 1], 1024 * h, 1024), A.is_lt)
+                    mm(o, [(ALL, l, True)] + ex)
+            if k < 2:
+                act(sub(sig, 128 * k, 128), pc, AF.Sign, bias=-8.5)
+        ts(has, pc, -7.5, None, A.is_gt)
+        pd = mm(psum(), [(I2, sub(sig, 0, 128), False), (I1, sub(sig, 128, 128), False)])
+        act(sub(T2, 0, 128), pd, AF.Relu, bias=1024.0, scale=-1024.0)
+        act(sub(T3, 0, 128), sub(T2, 0, 128), bias=8192.0)
+        op("V", vc(128, 0.5), [has], [hs],
+           lambda: g.vector.tensor_tensor_scan(ap(hs), ap(has), ap(has), 0.0, A.add, A.max), "scan")
+        pcum = mm(psum(), [(BD, hs, False)])
+        ppl = mm(psum(), [(BD, hs, False), (NUP, has, False)])
+        tt(sub(T1, 0, 128), ppl, has, A.mult)
+        nvs, colu = NVS[t], new("UU", 16)
+        if nvs:
+            ts(cb, pcum, 256.0, None, A.min)
+        for b in range(16):
+            jk, ac = reg("JK", 128 * b, 128), sub(acc, b, 1)
+            if b < nvs:
+                ts(jk, cb, sub(kb, b, 1), 0.5, A.is_lt, A.subtract)
+                op("V", vc(128, 1.0), [jk], [ac],
+                   lambda jk=jk, ac=ac: g.vector.tensor_reduce(ap(ac), ap(jk), AxisListType.X, A.add), "red")
+            else:
+                act(jk, pcum, AF.Sign, bias=sub(kb, b, 1), scale=-1.0, acc=ac)
+        for lo, n, s in ((0, nvs, 16.0), (nvs, 16 - nvs, 8.0)):
+            if n:
+                ts(sub(colu, lo, n), sub(acc, lo, n), s / 16.0, 64.0, A.mult, A.add)
+                act(sub(c16, lo, n), sub(acc, lo, n), bias=1024.0, scale=s)
+        vgather(G1, T1, colu, X1, A.is_equal)
+        vgather(G2, T3, colu, G1, A.mult)
+        pw = tolist(psum(16), [(RA, G1), (ALL, G2)], [(I1, c16)])
+        sd = reg("SD", 272 * t, 272)
+        offu = ts(new("UU", 16), pw, -8192.0, 0.0, A.add, A.max)
+        nv = ts(sub(sd, 256, 16), pw, 8000.0, 8192.0, A.is_lt, A.mult)
+        sgather(ER, reg("SR", 3 * t * M, 3 * M), offu)
+        pe = tolist(psum(16), [(R08, ER)])
+        sgather(sub(sd, 0, 256), XW, cp(new("UU", 16), pe))
+        tt(em, pe, nv, A.add)
+        rv, link = reg("RV%d" % t, 0, 272), ("link", t, t + 1, None)
+        op("G", 1.0, [sd], [link],
+           lambda t=t, sd=sd, rv=rv: g.remote_dma(ap(rv), ap(sd), T.sem["rv%d" % t], T.sem["sn%d" % t], peer[1], peer[0], peer[2]),
+           "send", lat=0.0, kind="r")
+        op(None, 0.0, [link], [rv], None, "recv", lat=2.5, kind="rv%d" % t)
+        tt(e3, em, sub(rv, 256, 16), A.add)
+        tt(e3, e3, tX, A.min)
+        scatter("V", XW, cp(new("UU", 16), e3), sub(rv, 0, 256))
+    dma("Y", [K[3]], [], [(lambda: T.yk[:], lambda: ap(K[3]))], 524288)
+    dma("Y", [Cn], [], [(lambda: T.yc[:], lambda: ap(Cn))], 65536)
+    yn = ("yn", 0, 1, None)
+    dma("G", [NWIN], [yn], [(lambda: T.yn[:], lambda: rows(NLO, 0, 16))], 131072, nrows=16)
+    dma("G", [NWIN], [yn], [(lambda h=h: T.yn[:, h:h + M], lambda h=h: rows(sub(NLO, h, M), 8, 16)) for h in (0, M)],
+        131072, nrows=16, accum_op=A.add)
+    dma("Y", [XW], [], [(lambda: T.yx[:], lambda: T.XX[:, 0:IT])], 1048576)
+    return ops, bank
+
+
+def depends(ops):
+    def clash(a, b):
+        return a[1] < b[2] and b[1] < a[2] and (a[3] is None or b[3] is None or a[3] == b[3])
+
+    seen = {}
+    for k, o in enumerate(ops):
+        dep = set()
+        for r in o["rd"]:
+            dep.update(j for j, q, w in seen.get(r[0], ()) if w and clash(r, q))
+        for r in o["wr"]:
+            dep.update(j for j, q, w in seen.get(r[0], ()) if clash(r, q))
+        for r in o["rd"]:
+            seen.setdefault(r[0], []).append((k, r, False))
+        for r in o["wr"]:
+            seen.setdefault(r[0], []).append((k, r, True))
+        dep.discard(k)
+        o["dep"] = sorted(dep)
+        o["pv"] = sorted(set(r[0] for r in o["rd"] + o["wr"] if isinstance(r[0], tuple)))
+
+
+def place(seq, pred, eng, dur, pre, post):
+    busy, st, fin = {e: [] for e in eng}, [0.0] * len(dur), [0.0] * len(dur)
+    for k in seq:
+        s, d = pre[k], dur[k]
+        if pred[k]:
+            s += max([fin[j] for j in pred[k]])
+        if d:
+            lst = busy[eng[k]]
+            i = n = len(lst)
+            while i and lst[i - 1][1] > s:
+                i -= 1
+            while i < n and s + d > lst[i][0]:
+                if lst[i][1] > s:
+                    s = lst[i][1]
+                i += 1
+            lst.insert(i, (s, s + d))
+        st[k], fin[k] = s, s + d + post[k]
+    return st, fin
+
+
+def deal(ops, seq, eng):
+    left, bank = {}, {}
+    for o in ops:
+        for v in o["pv"]:
+            left[v] = left.get(v, 0) + 1
+    holder, last = [None] * 8, [-1] * 8
+    pos, dep, order, rest = {}, {}, [], list(seq)
+    while rest:
+        for i, k in enumerate(rest):
+            o = ops[k]
+            if all(j in pos for j in o["dep"]) and (all(v in bank for v in o["pv"]) or None in holder):
+                break
+        else:
+            return None
+        del rest[i]
+        d = set(o["dep"])
+        for v in o["pv"]:
+            fresh = v not in bank
+            if fresh:
+                bank[v] = min((pos.get(last[b], -1), b) for b in range(8) if holder[b] is None)[1]
+                holder[bank[v]] = v
+            b = bank[v]
+            if last[b] >= 0 and (fresh or eng[last[b]] != eng[k]):
+                d.add(last[b])
+            last[b] = k
+            left[v] -= 1
+            if left[v] == 0:
+                holder[b] = None
+        pos[k] = len(order)
+        order.append(k)
+        dep[k] = d
+    return order, bank, dep
+
+
+def length(ops, order, dep, eng, m):
+    free, fin = {}, {}
+    for k in order:
+        o = ops[k]
+        d = o["dur"] * m.get(o["name"], m["c"] if o["eng"] in ("V", "S") else 1.0)
+        o["start"] = s = max([fin[j] for j in dep[k]] + [free.get(eng[k], 0.0)])
+        fin[k] = s + d + o["lat"] * (m["lat"] if o["kind"] == "c" else 1.0)
+        if o["eng"]:
+            free[eng[k]] = s + d
+    return max(fin.values())
+
+
+COSTS = [{"sg": a, "vg": a, "sc": b, "mm": c, "lat": d, "c": e} for a, b, c, d, e in
+         ((0.7, 0.5, 1.0, 1.0, 0.85), (1.3, 1.5, 1.0, 1.0, 1.1), (0.7, 1.5, 1.5, 2.0, 1.0), (1.3, 0.5, 0.7, 0.5, 1.0),
+          (0.8, 0.8, 1.7, 1.0, 0.8), (1.0, 1.0, 1.0, 1.0, 1.0))]
+WEIGHT = (110.0, 180.0, 160.0, 140.0, 130.0, 60.0)
+
+
+def schedule(ops):
+    n = len(ops)
+    pred, succ = [o["dep"] for o in ops], [[] for _ in ops]
+    for k in range(n):
+        for j in pred[k]:
+            succ[j].append(k)
+    eng, dur, lat, zero = [o["eng"] for o in ops], [o["dur"] for o in ops], [o["lat"] for o in ops], [0.0] * n
+
+    def run(key, eng):
+        for k in range(n):
+            for j in pred[k]:
+                if key[k] < key[j]:
+                    key[k] = key[j]
+        st, fin = place(sorted(range(n), key=lambda k: (key[k], k)), pred, eng, dur, zero, lat)
+        bs, bf = place(sorted(range(n), key=lambda k: (-fin[k], -k)), succ, eng, dur, lat, zero)
+        st, fin = place(sorted(range(n), key=lambda k: (-bf[k], k)), pred, eng, dur, zero, lat)
+        return max(fin), st
+
+    rng = np.random.RandomState(SEED)
+    cur, st = run([float(k) for k in range(n)], eng)
+    best, low, flex = None, cur, [k for k in range(n) if "alt" in ops[k]]
+    for it in range(TRIES):
+        key = list(st)
+        for _ in range(rng.randint(0, 3)):
+            a, w, d = rng.randint(n), rng.randint(1, 40), float(rng.randn()) * 8.0
+            for k in range(a, min(n, a + w)):
+                key[k] += d
+        e2 = list(eng)
+        if rng.rand() < 0.3:
+            k = flex[rng.randint(len(flex))]
+            e2[k] = "V" if e2[k] == "S" else "S"
+        m, s2 = run(key, e2)
+        if m < cur or rng.rand() < np.exp((cur - m) / (TEMP * (1.0 - it / TRIES) + 0.02)):
+            cur, st, eng = m, s2, e2
+            if m < low + 1.0 or best is None:
+                low = min(low, m)
+                got = deal(ops, sorted(range(n), key=lambda k: (st[k], k)), eng)
+                if got:
+                    ls = [length(ops, got[0], got[2], eng, c) for c in COSTS]
+                    sc = sum(x / w for x, w in zip(ls, WEIGHT))
+                    if best is None or sc < best[0]:
+                        best = (sc, got + (eng,), ls)
+    return best
+
+
+FOUND = []
+
+
+def rank_program(g, core, T, topo):
+    rank = T.rank_of(core)
+    if rank is None:
+        return
+    n = len(T.cores)
+    nxt, prv = T.cores[(rank + 1) % n], T.cores[(rank - 1) % n]
+    assert topo.may_write(core, nxt)
+    rid, pid, _ = topo.addr(nxt)
+    n_out, n_in = len(topo.engines(core, nxt)), len(topo.engines(prv, core))
+    ops, bank = plan(T, g, (rid, pid, topo.mask(core, nxt)))
+    depends(ops)
+    if not FOUND:
+        FOUND.append(schedule(ops)[1])
+    order, banks, dep, eng = FOUND[0]
+    for o, e in zip(ops, eng):
+        if e != o["eng"]:
+            o.update(eng=e, fn=o["alt"])
+    bank.update(banks)
+    pos = {k: i for i, k in enumerate(order)}
+    queue = {"V": g.vector, "S": g.scalar, "P": g.tensor, "G": g, "Y": g.sync}
+    known = {q: {} for q in queue}
+    count = {"V": 0, "S": 0, "P": 0, "G": 0}
+    nd, final = 0, {}
+    for k in order:
+        o = ops[k]
+        if o["eng"] is None:
+            o["tok"], o["clock"] = (o["kind"], n_in), {}
+            final[o["kind"]] = n_in
+            continue
+        kn = known[o["eng"]]
+        for j in sorted(dep[k], key=lambda j: -pos[j]):
+            s, v = ops[j]["tok"]
+            if kn.get(s, 0) < v:
+                queue[o["eng"]].wait_ge(T.sem[s], v)
+                kn[s] = v
+                for s2, v2 in ops[j]["clock"].items():
+                    kn[s2] = max(kn.get(s2, 0), v2)
+        o["clock"] = dict(kn)
+        r = o["fn"]()
+        if o["kind"] == "c":
+            count[o["eng"]] += 1
+            o["tok"] = ("c" + o["eng"], count[o["eng"]])
+            r.then_inc(T.sem[o["tok"][0]], 1)
+        elif o["kind"] == "d":
+            o["tok"] = ("d%d" % nd, o["inc"])
+            nd += 1
+            for x in r:
+                x.then_inc(T.sem[o["tok"][0]], 16)
+        else:
+            continue
+        final[o["tok"][0]] = o["tok"][1]
+    for t in range(RO):
+        final["sn%d" % t] = n_out
+    for s, v in final.items():
+        g.sync.wait_ge(T.sem[s], v)

@@ -1,34 +1,46 @@
 import numpy as np
-from concourse.mybir import AluOpType, AxisListType, ActivationFunctionType
+from concourse.mybir import AluOpType, ActivationFunctionType
 
 A = AluOpType
 AF = ActivationFunctionType
 IT, M, RO = 4096, 2048, 3
-SENT = IT + M
-KW, NW = M + 16, SENT + 16
+OFF = 16384.0
+SENT = IT
+KW, GW = M + 16, IT + 16
+NW, XW = GW + M, GW + 256
 
-SCRATCH = {"KK": 4 * KW, "XX": NW, "NN": NW, "GL": M, "LE": M, "LT": 3 * M, "PP": M, "ZR": M, "SR": 9 * M, "SB": M,
-           "W0": 2 * M, "JK": M, "SD": 3 * 272, "RV0": 272, "RV1": 272, "RV2": 272, "BB": 80 * 128}
+SCRATCH = {"KK": 4 * KW, "XX": XW, "NN": GW, "GL": M, "LE": M, "LT": 3 * M, "PP": M, "ZR": M, "QQ": M, "SR": 2 * M,
+           "SB": M, "W0": 4 * M, "EE": M, "SD": 3 * 272, "RV": 3 * 272, "BB": 80 * 128}
 SCRATCH = {k: ("sbuf", [128, n], "bfloat16") for k, n in SCRATCH.items()}
-SCRATCH.update({k: ("sbuf", [128, n], "float32") for k, n in (("SF", M), ("W1", 2 * M), ("W2", 2 * M), ("FF", 36 * 128))})
-SCRATCH.update({"II": ("sbuf", [128, 20 * 128], "int32"), "UU": ("sbuf", [128, 30 * 128], "uint16")})
+SCRATCH.update({k: ("sbuf", [128, n], "float32") for k, n in (("SF", M), ("NF", NW + GW), ("FF", 90 * 128))})
+SCRATCH.update({"II": ("sbuf", [128, 12 * 128], "int32"), "UU": ("sbuf", [128, 30 * 128], "uint16"),
+                "HH": ("sbuf", [128, 512], "float16")})
 SCRATCH.update({"PS%d" % k: ("psum", [128, 512], "float32") for k in range(8)})
-SEMAPHORES = ["cV", "cS", "cP", "cG"] + ["d%d" % k for k in range(40)] + ["rv0", "rv1", "rv2", "sn0", "sn1", "sn2"]
+SEMAPHORES = ["cV", "cS", "cP", "cG"] + ["d%d" % k for k in range(44)] + [s + str(k) for s in ("rv", "sn") for k in range(2 * RO)]
 
-WENG = ("V", "S", "S")
-XS = ((), (), ())
-NVS = (0, 0, 5)
-DCH = (64, 128, 128)
-NMS = 2560
-GCH, SCH = 1024, 512
-CY, GA, SC, PEC, LAT = 1.04e-3, 1.56, 3.8, 0.6e-3, 0.12
-SEED, TRIES, TEMP = 13, 11000, 0.45
-SIZE = {"float32": 4, "int32": 4, "bfloat16": 2, "uint16": 2}
+PAR = {"XS": ((), (), (1,)),
+       "NVE": (4, 4, 5),
+       "DCH": (64, 128, 128),
+       "LCH": (64, 128, 128),
+       "CLR": "VVVVVSSS VVVV SSGG",
+       "NMS": 4096,
+       "VCH": 1024, "GCH": 1024, "SCH": 512, "NCH": (512, 512, 512),
+       "TWO": (0,),
+       "DUE": dict([(s + str(t), d) for s, ds in (("M", (10, 24, 46)), ("K", (15, 38, 60)), ("W", (18, 36, 56)),
+                                                  ("P", (12, 40, 61)), ("Q", (21, 43, 64)), ("S", (27, 47, 68)),
+                                                  ("T", (32, 51, 72)), ("X", (26, 48, 72)), ("Y", (31, 52, 75)),
+                                                  ("Z", (36, 56, 78)), ("E", (45, 66, 89)), ("N", (38, 54, 90)),
+                                                  ("C", (90, 90, 90))) for t, d in enumerate(ds)]
+                   + [("O0", 95), ("A", 95), ("H0", 7), ("H1", 8), ("gap", 0.5), ("bias", 3.0)]),
+       "MERGE": False, "MARK": "W0 E0 Q1 E1 Q2 Z2", "PULL": 0.07, "MIDT": 0.01, "FLIP": (0.0, 0.05, 0.1), "LOOK": 0.5, "ROUGH": 1500, "SEED": 5, "TRIES": 38000, "TEMP": 0.01}
+CY, GA, SC, PEC, LAT = 1.0e-3, 1.3, 3.0, 0.52e-3, 0.12
+SIZE = {"float32": 4, "int32": 4, "bfloat16": 2, "uint16": 2, "float16": 2}
 
 
 def plan(T, g, peer):
-    ops, bank, npv = [], {}, [0]
-    top = {"FF": 0, "BB": 0, "II": 0, "UU": 0}
+    ops, bank, npv, step = [], {}, [0], ["A"]
+    top = {"FF": 0, "BB": 0, "II": 0, "UU": 0, "HH": 0}
+    GCH = PAR["GCH"]
 
     def new(b, n=128):
         lo = top[b]
@@ -49,6 +61,9 @@ def plan(T, g, peer):
     def isps(r):
         return isinstance(r[0], tuple)
 
+    def size(r):
+        return 4 if isps(r) else SIZE[SCRATCH[r[0]][2]]
+
     def ap(r):
         return T["PS%d" % bank[r[0]] if isps(r) else r[0]][:, r[1]:r[2]]
 
@@ -59,13 +74,17 @@ def plan(T, g, peer):
         return ap(s) if isinstance(s, tuple) else s
 
     def op(eng, dur, rd, wr, fn, name, lat=LAT, inc=1, kind="c"):
-        ops.append({"eng": eng, "dur": dur, "rd": rd, "wr": wr, "fn": fn, "lat": lat, "inc": inc, "kind": kind, "name": name})
+        ops.append({"eng": eng, "dur": dur, "rd": rd, "wr": wr, "fn": fn, "lat": lat, "inc": inc, "kind": kind, "name": name,
+                    "step": step[0]})
+
+    def at(name, t):
+        step[0] = name + str(t)
 
     def vc(n, f):
         return 0.05 + max(64, n * f) * CY
 
     def half(*rs):
-        return 0.5 if all(not isps(r) and SIZE[SCRATCH[r[0]][2]] == 2 for r in rs) else 1.0
+        return 0.5 if all(size(r) == 2 for r in rs) else 1.0
 
     def ts(o, i, s1, s2, o0, o1=None):
         rd = [i] + [s for s in (s1, s2) if isinstance(s, tuple)]
@@ -89,13 +108,10 @@ def plan(T, g, peer):
         op("V", vc(o[2] - o[1], half(o)), [], [o], lambda: g.vector.memset(ap(o), float(c)), "ms")
         return o
 
-    def act(o, i, fn=AF.Identity, bias=0.0, scale=1.0, acc=None):
+    def act(o, i, fn=AF.Identity, bias=0.0, scale=1.0):
         rd = [i] + [s for s in (bias, scale) if isinstance(s, tuple)]
-        if acc is None:
-            f = lambda: g.scalar.activation(ap(o), ap(i), fn, bias=val(bias), scale=val(scale))
-        else:
-            f = lambda: g.scalar.activation(ap(o), ap(i), fn, bias=val(bias), scale=val(scale), accum_out=ap(acc))
-        op("S", 0.07 + max(64, i[2] - i[1]) * CY, rd, [o] + ([acc] if acc else []), f, "act")
+        op("S", 0.07 + max(64, i[2] - i[1]) * CY, rd, [o],
+           lambda: g.scalar.activation(ap(o), ap(i), fn, bias=val(bias), scale=val(scale)), "act")
         return o
 
     def iota(o, pat, base, cm):
@@ -109,6 +125,11 @@ def plan(T, g, peer):
     def fill(o, c):
         return iota(o, [[0, o[2] - o[1]]], c, 0)
 
+    def keep(o, i, pat, how, c, base, cm):
+        op("G", 0.17 + 2 * (o[2] - o[1]) * CY, [i], [o],
+           lambda: g.affine_select(ap(o), ap(i), pat, how, float(c), base, cm), "iota")
+        return o
+
     def chunks(n, c):
         return [(lo, min(c, n - lo)) for lo in range(0, n, c)]
 
@@ -120,13 +141,13 @@ def plan(T, g, peer):
             ops[-1]["alt"] = lambda oo=oo, ff=ff: g.vector.tensor_copy(ap(oo), ap(win).indirect(ap(ff)))
 
     def vgather(o, win, off, in1, o0):
-        for lo, n in chunks(o[2] - o[1], GCH):
+        for lo, n in chunks(o[2] - o[1], PAR["VCH"]):
             oo, ff, i1 = sub(o, lo, n), sub(off, lo // 16, n // 16), sub(in1, lo, n)
             op("V", 0.05 + n * GA * CY, [win, ff, i1], [oo],
                lambda oo=oo, ff=ff, i1=i1: g.vector.tensor_tensor(ap(oo), ap(win).indirect(ap(ff)), ap(i1), o0), "vg")
 
-    def scatter(eng, win, off, src):
-        for lo, n in chunks(src[2] - src[1], SCH):
+    def scatter(eng, win, off, src, ch):
+        for lo, n in chunks(src[2] - src[1], ch):
             ss, ff = sub(src, lo, n), sub(off, lo // 16, n // 16)
             f = fv = lambda ss=ss, ff=ff: g.vector.tensor_copy(ap(win).indirect(ap(ff)), ap(ss))
             if eng == "S":
@@ -135,278 +156,397 @@ def plan(T, g, peer):
             if eng == "S":
                 ops[-1]["alt"] = fv
 
-    def mm(o, terms):
-        rd, cnt = [], 0
-        for l, r, st in terms:
-            rd += [l, r]
-            cnt += 16 if st else 1
+    def mm(o, lists=(), terms=()):
+        n = max(64, o[2] - o[1])
+        cyc = 16 * n * len(lists) + sum(n * (4 if size(r) == 4 else 1) for l, r in terms)
 
         def f():
             pairs = []
-            for l, r, st in terms:
-                if st:
-                    pairs += [(T[l[0]][:, l[1] + 16 - i:l[1] + 144 - i], T[r[0]][:, r[1] + i:r[2]:16]) for i in range(16)]
-                else:
-                    pairs.append((ap(l), ap(r)))
-            return [g.tensor.matmul(ap(o), l, r, k == 0, k == cnt - 1) for k, (l, r) in enumerate(pairs)][-1]
-        op("P", 0.06 + cnt * max(64, o[2] - o[1]) * PEC, rd, [o], f, "mm")
+            for l, r in lists:
+                pairs += [(T[l[0]][:, l[1] + 16 - i:l[1] + 144 - i], T[r[0]][:, r[1] + i:r[2]:16]) for i in range(16)]
+            pairs += [(ap(l), ap(r)) for l, r in terms]
+            return [g.tensor.matmul(ap(o), l, r, k == 0, k == len(pairs) - 1) for k, (l, r) in enumerate(pairs)][-1]
+        op("P", 0.06 + cyc * PEC, [x for p in list(lists) + list(terms) for x in p], [o], f, "mm")
         return o
 
-    def tolist(o, terms, extra=()):
-        for lo, n in chunks(terms[0][1][2] - terms[0][1][1], GCH):
-            mm(sub(o, lo // 16, n // 16), [(s, sub(tab, lo, n), True) for s, tab in terms]
-               + [(l, sub(r, lo // 16, n // 16), False) for l, r in extra])
+    def tolist(o, lists, terms=(), ch=64):
+        for lo, n in chunks(o[2] - o[1], ch):
+            mm(sub(o, lo, n), [(s, sub(tab, 16 * lo, 16 * n)) for s, tab in lists], [(l, sub(r, lo, n)) for l, r in terms])
         return o
 
-    def dma(q, rd, wr, pairs, nbytes, nrows=128, **kw):
+    def dma(q, rd, wr, pairs, nbytes, nrows=128, after=(), turn=False):
         e = {"Y": g.sync, "S": g.scalar, "G": g}[q]
-        op(q, {"Y": 0.1, "S": 0.1, "G": 1.0}[q] * len(pairs), rd, wr, lambda: [e.dma_start(o(), i(), **kw) for o, i in pairs],
-           "dma", lat=2.0 + nbytes / 250e3 + nrows * 0.004, inc=16 * len(pairs), kind="d")
+        link, done = ("dma", len(ops), len(ops) + 1, None), ("done", len(ops), len(ops) + 1, None)
+        op(q, {"Y": 0.2, "S": 0.15, "G": 1.6}[q] * len(pairs), rd + list(after), wr + [link] + [("turn" + q, 0, 1, None)] * turn,
+           lambda: [e.dma_start(o(), i()) for o, i in pairs], "dma", inc=16 * len(pairs), kind="d")
+        op("D", nbytes / 320e3 + nrows * 0.0015, rd + [link], wr + [done] + [("turn", 0, 1, None)] * turn, None, "move",
+           lat=0.5 if q == "G" else 0.0, kind="m")
+        return done
 
-    def load(q, name, r, nbytes=65536):
-        dma(q, [], [r], [(lambda: ap(r), lambda: T[name][:])], nbytes)
+    def load(q, name, r, nbytes=65536, after=()):
+        dma(q, [], [r], [(lambda: ap(r), lambda: T[name][:])], nbytes, after=after, turn=not after)
         return r
 
-    def torow(q, tab, row, lst):
-        dma(q, [lst], [sub(tab, 0, tab[2] - tab[1], "r%d" % row)], [(lambda: rows(tab, row, 16), lambda: ap(lst))], 65536)
+    def torow(q, tab, hi, lo):
+        return dma(q, [hi, lo], [tab], [(lambda: rows(tab, 0, 16), lambda: ap(hi)), (lambda: rows(tab, 8, 16), lambda: ap(lo))],
+                   65536, nrows=256)
+
+    def copy(o, i):
+        return dma("Y", [i], [o], [(lambda: ap(o), lambda: ap(i))], 524288)
+
+    def send(k, src, dst):
+        link = ("link", k, k + 1, None)
+        op("G", 1.0, [src], [link],
+           lambda: g.remote_dma(ap(dst), ap(src), T.sem["rv%d" % k], T.sem["sn%d" % k], peer[1], peer[0], peer[2]),
+           "send", lat=0.0, kind="r")
+        op("D", 0.2 + 0.2 * (k % 2), [link], [dst], None, "recv", lat=2.5, kind="rv%d" % k)
 
     K = [reg("KK", t * KW, M) for t in range(4)]
     KWIN = [reg("KK", t * KW, KW) for t in range(4)]
     kl = load("Y", "kl", new("II"))
     kr = load("S", "kr", new("II"))
-    load("Y", "ky", K[0], 524288)
     nx = load("S", "nxt", new("II", 256), 131072)
-    cur, siz, tgt, par = [load("Y", n, new("II")) for n in ("cur", "siz", "tgt", "par")]
-    SB, SF = reg("SB", 0, M), reg("SF", 0, M)
-    load("Y", "ky", SB, 1048576)
-    load("Y", "x", reg("XX", 0, IT), 2097152)
-    XW, NWIN, NLO = reg("XX", 0, NW), reg("NN", 0, NW), reg("NN", 0, IT)
+    load("Y", "ky", K[0], 524288)
+    tgt, par, siz, cur = [load("Y", n, new("II")) for n in ("tgt", "par", "siz", "cur")]
+    XG, XS_, NLO = reg("XX", 0, GW), reg("XX", 0, XW), reg("NN", 0, IT)
+    NG = [reg("NN", 0, GW), reg("NF", 0, GW), reg("NF", NW, GW)]
+    NS = [reg("NF", 0, NW), reg("NF", GW, NW), reg("NF", GW, NW)]
 
     X1 = iota(new("FF", 256), [[1, 256]], 1, 0)
     pi = iota(new("II", 1), [[0, 1]], 0, 1)
     pf = iota(new("FF", 1), [[0, 1]], 0, 1)
-    p1 = iota(new("FF", 1), [[0, 1]], 1, 1)
-    vp = iota(new("FF"), [[16, 128]], 0, 1)
-    dh = iota(new("BB"), [[0, 128]], 128 * 128, 128)
-    dh0 = iota(new("BB"), [[0, 128]], 96 * 128, 128)
-    dl = iota(new("BB"), [[1, 128]], 128, 0)
-    ai = ts(new("II", 1), pi, 15, None, A.bitwise_and)
-    a7 = ts(new("II", 1), pi, 7, None, A.bitwise_and)
-    g16 = tt(new("FF", 1), pf, ai, A.subtract)
-    g17 = ts(new("FF", 1), g16, 17.0, None, A.add)
-    x144, x128 = sub(X1, 0, 144), sub(X1, 0, 128)
-    ALL = ts(new("BB", 144), x144, g17, None, A.is_equal)
-    m4 = ts(new("FF", 1), ai, 4.0, 8192.0, A.is_equal, A.mult)
-    m08 = ts(new("FF", 1), a7, 0.0, None, A.is_equal)
-    m2 = ts(new("FF", 1), ai, 2.0, 16.0, A.is_equal, A.mult)
-    m082 = tt(new("FF", 1), m2, m08, A.add)
-    m412 = ts(new("FF", 1), a7, 4.0, None, A.is_equal)
-    AP8, AN8, R4, R08, R2, R082, R412 = [act(new("BB", 144), ALL, scale=s) for s in (8192.0, -8192.0, m4, m08, m2, m082, m412)]
-    I1 = ts(new("BB"), x128, p1, None, A.is_equal)
-    I2, I8, IB, IQ, IZ, IG = [act(new("BB"), I1, scale=s) for s in (2.0, 8.0, -262144.0, -4096.0, 4096.0, -524288.0)]
-    b1 = ts(new("BB"), x128, g16, None, A.is_gt)
-    b2 = ts(new("BB"), x128, g17, None, A.is_lt)
-    BD = tt(new("BB"), b1, b2, A.mult)
-    b3 = ts(b2, x128, pf, -1.0, A.is_le, A.mult)
-    NUP = tt(new("BB"), b1, b3, A.mult)
-    cq = ts(new("FF", 1), g16, -128.0, -16512.0, A.mult, A.add)
-    CQ = act(new("BB"), x128, bias=cq, scale=0.0)
-    C2, C17, CM1 = fill(new("BB"), 2), fill(new("BB"), 17), fill(new("BB"), -1)
-    if any(XS):
-        AH = act(new("BB", 144), ALL, scale=0.5)
-        IN1, IN8 = act(new("BB"), I1, scale=-1.0), act(new("BB"), I1, scale=-8.0)
-    vm = ts(new("FF"), vp, g16, -float(M), A.subtract, A.add)
-    tN = act(new("FF"), vm, bias=float(IT + M))
-    kb = act(new("FF", 16), sub(vm, 0, 16), bias=0.5 + M)
-    tX = sub(tN, 0, 16)
-    RA = act(new("BB", 144), ALL, scale=cp(new("FF", 1), ai))
-    for t in range(3):
+    for t in range(4):
         fill(reg("KK", t * KW + M, 16), 255)
-    for lo in range(0, IT, 512):
-        (ms if lo < NMS else fill)(reg("NN", lo, 512), 0)
-    for lo, n in chunks(NW - IT, 256):
-        act(reg("NN", IT + lo, n), sub(X1, 0, n), bias=SENT / 2.0, scale=0.0)
-    W = [reg("W%d" % t, 0, 2 * M) for t in range(3)]
-    WU = [reg("W%d" % t, M, M) for t in range(3)]
-    for lo in range(0, M, 512):
-        fill(sub(WU[0], lo, 512), 0)
-    for t in range(3):
-        torow("G" if t else "Y", WU[t], 0, dh0)
-        torow("G" if t else "Y", WU[t], 8, dl)
-    torow("Y", SB, 0, dh)
-    torow("Y", SB, 8, dl)
-    dma("G", [SB], [SF], [(lambda: ap(SF), lambda: ap(SB))], 1048576)
-    for lo, n in chunks(NW - IT, 512):
-        fill(reg("XX", IT + lo, n), 255)
-    T1, T2 = new("FF", 144), new("BB", 144)
-    fill(sub(T1, 128, 16), 0)
+    ZERO, ONE = fill(new("FF", 144), 0), fill(new("BB", 144), 1)
+    vp = iota(new("FF"), [[16, 128]], 0, 1)
 
-    nh = cp(new("BB", 256), nx)
-    nl = tt(new("BB", 256), nx, nh, A.subtract)
-    torow("Y", NLO, 0, nh)
-    torow("Y", NLO, 8, nl)
+    def diag(o, c):
+        return keep(o, sub(ZERO, 0, 128), [[-1, 128]], A.not_equal, c, 0, 1)
+
+    def picks(rs, c):
+        o = new("BB", 144)
+        for k, r in enumerate(rs):
+            keep(o, o if k else ZERO, [[-16, 9], [-256, 16]], A.not_equal, c, 16 - r, 1)
+        return o
+
+    ALL = keep(new("BB", 144), ONE, [[-16, 9], [-256, 16]], A.is_ge, 0.0, 16, 1)
+    keep(ALL, ALL, [[16, 9], [0, 16]], A.is_ge, 0.0, -1, -1)
+    R4, R08, R412 = picks((4,), 1.0), picks((0, 8), 1.0), picks((4, 12), 1.0)
+    I1, IN, IK, IZ, IQ, I8, IE, IG, IX = [diag(new("BB"), s) for s in
+                                          (1.0, -1.0, 2048.0, 4096.0, -4096.0, 8.0, -8192.0, 2.0 ** 24, -32768.0)]
+    F1, FN = diag(new("FF"), 1.0), diag(new("FF"), -1.0)
+    dh, dl = iota(new("BB"), [[0, 128]], 128 * 128, 128), iota(new("BB"), [[1, 128]], 128, 0)
+    C6K = fill(new("BB"), 6144 - int(OFF))
+    KI = iota(new("BB", 256), [[1, 16], [16, 16]], 0, 0)
+    BD = keep(new("BB"), sub(ONE, 0, 128), [[-16, 8], [0, 16]], A.is_ge, 0.0, 0, 1)
+    keep(BD, BD, [[16, 8], [0, 16]], A.is_ge, 0.0, 15, -1)
+    NUP = fill(new("BB"), -1)
+    keep(NUP, NUP, [[16, 8], [0, 16]], A.is_ge, 0.0, 15, -1)
+    keep(NUP, NUP, [[-1, 128]], A.is_ge, 0.0, -1, 1)
+    GI = keep(new("BB", 8), sub(ONE, 0, 8), [[-16, 8]], A.is_ge, 0.0, 0, 1)
+    keep(GI, GI, [[16, 8]], A.is_ge, 0.0, 15, -1)
+    offe = {n: keep(o, fill(o, 128), [[0, 1]], A.is_ge, 0.0, -16 * n, 1) for n in sorted(set(PAR["NVE"])) for o in [new("FF", 1)]}
+    ALH = cp(new("HH", 144), ALL)
+    ng = tt(new("FF", 1), ts(new("II", 1), pi, 15, None, A.bitwise_and), pf, A.subtract)
+    vv = act(new("FF"), vp, bias=ng)
+    tN = act(new("FF"), vv, bias=float(GW))
+    tO = act(new("FF"), vv, bias=OFF - M)
+    tX = sub(tN, 0, 16)
+    cq = act(new("FF", 1), ng, bias=-16512.0, scale=128.0)
+    cG = act(new("FF"), vv, bias=cq, scale=-1.0)
+    if any(PAR["XS"]):
+        AH = act(new("BB", 144), ALL, scale=0.5)
+    SB, SF = reg("SB", 0, M), reg("SF", 0, M)
+    W = [reg("W0", 0, 3 * M), reg("W0", 0, 4 * M)]
+    WA, WB = reg("W0", 2 * M, M), reg("W0", 3 * M, M)
+    for tab, way in zip((NLO, SB, WA), PAR["CLR"].split()):
+        for k, e in enumerate(way):
+            o = sub(tab, 512 * k, 512)
+            fill(o, 0) if e == "G" else ms(o, 0) if e == "V" else act(o, reg("NN", 0, 512), AF.Copy)
+    at("H", 1)
+    torow("Y", SB, dh, dl)
+    wa = torow("Y", WA, dh, dl)
+    at("A", "")
+    fill(reg("NN", IT, 16), 32768)
+    fill(reg("XX", IT, 16), 255)
+    T1, T3 = new("FF", 144), new("FF", 144)
+    fill(sub(T1, 128, 16), 0)
+    fill(sub(T3, 128, 16), 0)
+
+    nh = ts(new("BB", 256), nx, OFF - 192.0, None, A.add)
+    nl = act(new("BB", 256), tt(new("FF", 256), nx, nh, A.subtract), bias=OFF)
+    nhf, nlf = new("FF", 256), new("FF", 256)
+    at("H", 0)
+    na = torow("Y", NLO, nh, nl)
+    at("A", "")
+    load("Y", "x", reg("XX", 0, IT), 1048576, after=[na, wa])
     zh = cp(new("BB"), siz)
     zl = tt(new("BB"), siz, zh, A.subtract)
     zp = psum(256)
-    mm(sub(zp, 0, 128), [(zh, I1, False)])
-    mm(sub(zp, 128, 128), [(zl, I1, False)])
+    mm(sub(zp, 0, 128), terms=[(zh, I1)])
+    mm(sub(zp, 128, 128), terms=[(zl, I1)])
     zt = act(new("BB", 256), zp, AF.Copy)
     ZR = reg("ZR", 0, M)
     dma("Y", [zt], [ZR], [(lambda k=k: T.ZR[16 * (k % 8) + 4 + 8 * (k // 8):16 * (k % 8) + 5 + 8 * (k // 8), :],
-                           lambda k=k: ap(sub(zt, 16 * k, 16))) for k in range(16)], 65536, nrows=2048)
+                           lambda k=k: ap(sub(zt, 16 * k, 16))) for k in range(16)], 65536, nrows=1024)
+    for lo in range(0, M, 512):
+        fill(sub(SF, lo, 512), 0)
+        if PAR["MERGE"]:
+            fill(sub(WB, lo, 512), 0)
+    if PAR["MERGE"]:
+        torow("Y", WB, dh, dl)
+    for tab in NG[1:]:
+        for lo, n in chunks(GW, 688):
+            fill(sub(tab, lo, n), 0)
 
     klu, kru = cp(new("UU"), kl), cp(new("UU"), kr)
+    cV, kh = ts(new("FF"), kl, 2.0 * M, None, A.add), new("FF", 256)
+    tt(sub(kh, 0, 128), kr, kl, A.subtract)
+    kv = tt(sub(kh, 128, 128), vv, cV, A.subtract)
     T1p = tt(new("FF"), tgt, par, A.mult)
     T0p = tt(new("FF"), tgt, T1p, A.subtract)
     room = tt(new("FF"), T0p, siz, A.subtract)
-    nwl = [ts(new("BB"), room, 0.5, None, A.is_lt), tt(new("BB"), siz, T1p, A.is_ge), None]
-    nwd = [None, act(new("BB"), T1p, AF.Relu, bias=1.0, scale=-1.0), act(new("BB"), T0p, AF.Relu, bias=1.0, scale=-1.0)]
+    par0 = ts(new("BB"), par, -1.0, 1.0, A.mult, A.add)
+    nwl = [ts(new("BB"), room, 0.5, 64.0, A.is_lt, A.mult), tt(new("BB"), siz, T1p, A.is_ge)]
+    nwd = [None, act(new("BB"), T1p, AF.Relu, bias=64.0, scale=-64.0), act(new("BB"), T0p, AF.Relu, bias=64.0, scale=-64.0)]
+    rm = act(new("FF"), mm(psum(), terms=[(F1, room), (IZ, nwd[2])]), AF.Copy)
     c0 = ts(new("FF"), siz, 0.5, float(SENT), A.is_lt, A.mult)
     Cf = tt(c0, c0, cur, A.max)
     Cu = cp(new("UU"), Cf)
-    Cn = ts(new("FF"), cur, 8192.0, None, A.add)
-    PPr, GL, LE = reg("PP", 0, M), reg("GL", 0, M), reg("LE", 0, M)
-    has, hs, sig, cb = new("BB"), new("BB"), new("BB", 384), new("BB")
-    G1, G2, ER = new("BB", 256), new("BB", 256), new("BB", 256)
-    acc, e3, em, c16 = new("FF", 16), new("FF", 16), new("FF", 16), new("BB", 16)
-    T3 = new("BB", 144)
-    fill(sub(T3, 128, 16), 0)
-    kept = gone = S3p = None
+    Cn = ts(new("FF"), cur, 8192.0 + OFF, None, A.add)
+    PPr, GL, LE, EE = reg("PP", 0, M), reg("GL", 0, M), reg("LE", 0, M), reg("EE", 0, M)
+    has, hs, sig = new("BB"), new("BB"), new("BB", 256)
+    G1, G2 = new("BB", 256), new("HH", 256)
 
-    for t in range(RO):
-        pen = [nwl[0]] if t == 0 else [nwd[t], tt(new("BB"), nwl[t], kept, A.min)]
+    def part(terms, lo, n):
+        return [(l, sub(r, lo, n)) for l, r in terms]
+
+    def choose(t, pen):
+        at("M", t)
         sgather(GL, KWIN[t], klu)
         vgather(LE, KWIN[t], kru, GL, A.is_ge)
-        emp = act(new("BB"), tolist(psum(), [(R4, GL)]), AF.Relu, bias=-254.0, scale=1.0 / 8192.0)
-        a2, cr, owu = new("FF"), new("FF"), new("UU")
-        for lo, n in chunks(128, DCH[t]):
-            le = sub(LE, 16 * lo, 16 * n)
-            pl = tolist(psum(n), [(AP8, le)], [(IQ, C17)] + [(IB, sub(x, lo, n)) for x in pen + [emp]])
-            pr = tolist(psum(n), [(AN8, le)], [(IZ, C17)] + [(IB, sub(x, lo, n)) for x in pen])
-            a, c = sub(a2, lo, n), sub(cr, lo, n)
-            tt(a, pl, sub(kl, lo, n), A.min)
-            tt(c, pr, sub(kr, lo, n), A.min)
-            tt(a, a, sub(vm, lo, n), A.max)
-            tt(a, a, c, A.max)
-            ts(sub(owu, lo, n), a, float(M), None, A.add)
-        gs = act(new("BB"), a2, AF.Sign, bias=0.5)
-        if t > 0:
-            pg = mm(psum(), [(I8, gone, False), (IG, gs, False), (IB, C2, False)])
-        if t < 2:
-            base = ts(new("II"), a2, float(M), None, A.add)
-            ts(base, base, M - 1, None, A.bitwise_and)
-            if t > 0:
-                tt(base, pg, base, A.max)
-            sgather(K[t + 1], KWIN[t], ts(new("UU"), base, float(M), None, A.min))
-        if t == 0:
-            scatter("V", W[0], owu, SB)
+        emp = act(new("BB"), tolist(psum(), [(R4, GL)]), AF.Relu, bias=-254.0 * 4, scale=4.0)
+        ss, tl = new("BB", 256), new("FF", 256)
+        sr, sn = sub(ss, 0, 128), sub(ss, 128, 128)
+        for lo, n in chunks(128, PAR["DCH"][t]):
+            c = lambda r: sub(r, lo, n)
+            pl = tolist(psum(n), [(ALL, sub(LE, 16 * lo, 16 * n))], [(I1, c(x)) for x in pen + [emp]])
+            ts(c(sr), pl, 8.5, None, A.is_lt)
+            ts(c(sn), pl, 16.5, None, A.is_gt)
+            if n == 128:
+                tt(tl, ss, kh, A.mult)
+            else:
+                tt(c(tl), c(sr), c(kh), A.mult)
+                tt(sub(tl, 128 + lo, n), c(sn), sub(kh, 128 + lo, n), A.mult)
+        return sn, [(F1, sub(tl, 0, 128)), (F1, sub(tl, 128, 128))]
+
+    def cast(o, terms, s1, s2=None, ch=128):
+        for lo, n in chunks(128, ch):
+            ts(sub(o, lo, n), mm(psum(n), terms=part(terms, lo, n)), s1, s2, *((A.add, A.min) if s2 else (A.add,)))
+        return o
+
+    def keys(t, terms, s1):
+        sgather(K[t + 1], KWIN[t], cast(new("UU"), terms, s1, float(M), PAR["DCH"][t]))
+
+    for t in range(RO):
+        ptu = new("UU")
+        if t == 0 or not PAR["MERGE"]:
+            at("M", t)
+            pen = [nwl[0]] if t == 0 else [nwd[t], act(new("BB"), mm(psum(), terms=[(I1, (nwl[1], cond)[t - 1]), (IN, gone)]),
+                                                       AF.Relu, scale=64.0)]
+            sn, step0 = choose(t, pen)
+            owu, of, pf_ = new("UU"), new("FF"), new("FF")
+            for lo, n in chunks(128, PAR["DCH"][t]):
+                po = mm(psum(n), terms=part([(F1, cV)] + step0, lo, n))
+                cp(sub(owu, lo, n), po)
+                act(sub(of, lo, n), po, AF.Copy)
+            at("K", t)
+            mine = [(F1, of), (IZ, sn)]
+            keys(t, mine + ([(I1, tt(new("BB"), sn, gone, A.mult))] if t else []), -4096.0)
+            at("W", t)
+            if t:
+                torow("Y", WA, dh, dl)
+            scatter("V", W[0], owu, SB, PAR["SCH"])
+            for lo, n in chunks(128, 64):
+                pq = mm(psum(n), [(R08, sub(WA, 16 * lo, 16 * n))], part(mine + [(F1, cG)], lo, n))
+                ts(sub(ptu, lo, n), pq, -4096.0, None, A.add)
+                act(sub(pf_, lo, n), pq, AF.Copy)
+            gone = act(new("BB"), mm(psum(), terms=[(F1, pf_), (FN, of), (IQ, sn)]), AF.Abs, scale=4096.0)
+        elif t == 1:
+            at("M", 1)
+            pen = act(new("BB"), mm(psum(), terms=[(I1, nwl[1]), (IN, gone)]), AF.Relu, scale=64.0)
+            sn, step1 = choose(1, [nwd[1], pen])
+            at("K", 1)
+            mine = [(F1, cV), (IZ, sn)] + step1
+            keys(1, mine + [(I1, tt(new("BB"), sn, gone, A.mult))], -4096.0)
+            at("M", 2)
+            both = act(new("FF"), mm(psum(), terms=[(F1, cV), (FN, kv), (IK, cond)] + step1), AF.Copy)
+            sn2, step2 = choose(2, [nwd[2]])
+            at("W", 1)
+            owu = cast(new("UU"), [(F1, both)] + step2, 0.0, None, PAR["DCH"][2])
+            mine = [(F1, act(new("FF"), mm(psum(), terms=mine), AF.Copy))]
+            torow("Y", WA, dh, dl)
+            scatter("V", W[1], owu, SB, PAR["SCH"])
+            pa0, paf = new("FF"), new("FF")
+            for lo, n in chunks(128, 64):
+                pa = mm(psum(n), [(R08, sub(WA, 16 * lo, 16 * n))], [(F1, sub(cG, lo, n))])
+                tt(sub(pa0, lo, n), pa, sub(par0, lo, n), A.mult)
+                act(sub(paf, lo, n), pa, AF.Copy)
+            cast(ptu, [(F1, pa0)] + mine, -4096.0, None, 64)
+            gone = act(new("BB"), pa0, AF.Abs, scale=4096.0)
         else:
-            scatter(WENG[t], W[t], owu, SF)
-            dma("G", [W[t]], [WU[0]], [(lambda: rows(WU[0], 0, 8), lambda t=t: rows(WU[t], 0, 8))], 65536, nrows=16)
-        pq = tolist(psum(), [(R08, WU[0])], [(I1, CQ), (IQ, gs)])
-        xi = tt(new("II"), pq, a2, A.max)
-        gone = act(new("BB"), pq, AF.Relu, bias=-3000.0)
-        if t < 2:
-            kept = act(new("BB"), pq, AF.Relu, bias=3000.0, scale=-1.0)
-        tks = act(new("BB"), pq, AF.Sign, bias=-3000.0)
-        if t == 2:
-            sgather(K[t + 1], KWIN[t], ts(new("UU"), tt(new("FF"), pg, xi, A.max), float(M), None, A.min))
-        ptu = cp(new("UU"), ts(new("II"), xi, M - 1, None, A.bitwise_and))
-        Q, S2, S3 = [reg("SR", (3 * t + k) * M, M) for k in range(3)]
-        sgather(PPr, NWIN, Cu)
+            at("W", 2)
+            go = ts(new("BB"), mm(psum(), terms=[(IG, sn2), (IK, cond), (IN, gone)]), 0.5, None, A.is_lt)
+            mine = [(F1, vv), (IQ, go), (F1, tt(new("FF"), mm(psum(), terms=[(FN, kv)] + step2), go, A.mult))]
+            at("K", 2)
+            keys(2, mine + [(I1, gone), (IN, tt(new("BB"), go, gone, A.mult))], 0.0)
+            at("W", 2)
+            pb = tolist(psum(), [(R08, WB)], [(F1, cG)], ch=128)
+            pbf, gb = act(new("FF"), pb, AF.Copy), act(new("BB"), pb, AF.Sign)
+            act(gb, gb, AF.Abs)
+            ga = act(new("BB"), mm(psum(), terms=[(F1, paf), (FN, pa0)]), AF.Abs, scale=4096.0)
+            cast(ptu, [(F1, pbf), (F1, paf), (FN, pa0)] + mine, 0.0)
+        at("P", t)
+        Q, S2, S3 = reg("QQ", 0, M), reg("SR", 0, M), reg("SR", M, M)
+        old = NG[t]
+        sgather(PPr, old, Cu)
+        hv = act(new("FF"), tolist(psum(), [(R08, PPr)]), AF.Copy)
         if t == 0:
             dma("Y", [ZR], [PPr], [(lambda: rows(PPr, 4, 8), lambda: rows(ZR, 4, 8))], 65536, nrows=16)
+        at("Q", t)
         sgather(Q, PPr, ptu)
-        pk = tolist(psum(), [(R2, Q)] + ([(R082, S3p)] if t else []), [(IQ, tks), (IQ, gs)])
-        du = cp(new("UU"), tt(new("FF"), pk if t else tt(new("FF"), pk, Cf, A.max), tN, A.min))
-        S3p = S3
         su = [new("UU") for _ in range(3)]
-        for lo, n in chunks(M, GCH):
-            p = mm(psum(n // 16), [(R08, sub(Q, lo, n), True), (I8, sub(gone, lo // 16, n // 16), False)])
-            ts(sub(su[0], lo // 16, n // 16), p, float(SENT), None, A.min)
+        sf = [new("FF") for _ in range(3)]
+        D, dab, dk, e = new("FF"), new("FF"), new("BB"), new("BB")
+        if t == 2 and PAR["MERGE"]:
+            hx = act(new("FF"), mm(psum(), terms=[(FN, hv), (IX, gb), (IX, gb)]), bias=-65536.0, scale=-1.0)
+            gone = ga
+        for lo, n in chunks(128, 64):
+            c = lambda r: sub(r, lo, n)
+            if t < 2 or not PAR["MERGE"]:
+                p = tolist(psum(n), [(R08, sub(Q, 16 * lo, 16 * n))], [(I1, c(gone))])
+                ts(c(su[0]), p, -OFF, float(SENT), A.add, A.min)
+                act(c(sf[0]), p, AF.Copy)
+                continue
+            p = tolist(psum(n), [(R08, sub(Q, 16 * lo, 16 * n))], [(I1, c(ga)), (IX, c(gb))])
+            tt(c(sf[0]), p, c(hx), A.max)
+            ts(c(su[0]), c(sf[0]), -OFF, float(SENT), A.add, A.min)
+        for lo, n in chunks(128, PAR["LCH"][t]):
+            c = lambda r: sub(r, lo, n)
+            p = mm(psum(n), terms=[(F1, c(hv)), (FN, c(sf[0])), (I1, c(gone))])
+            act(c(dab), p, AF.Abs)
+            ts(c(dk), c(dab), float(IT), None, A.is_lt)
+            tt(c(D), p, c(dk), A.mult)
+            act(c(dab), c(D), AF.Abs)
+        at("N", t)
         if t == 0:
-            gz = act(new("FF"), tolist(psum(), [(R412, Q)], [(IZ, gs), (IZ, CM1)]), AF.Relu)
-            nwl[2] = tt(new("BB"), gz, room, A.is_ge)
-        scatter("V", NWIN, du, Q)
-        Cf = new("FF")
-        for k, tab in ((1, S2), (2, S3)):
-            sgather(tab, NWIN, su[k - 1])
-            for lo, n in chunks(M, GCH):
-                p = mm(psum(n // 16), [(R08 if k == 1 else R082, sub(tab, lo, n), True)])
-                ts(sub(su[k], lo // 16, n // 16), p, float(SENT), None, A.min)
-                if k == 2:
-                    act(sub(Cf, lo // 16, n // 16), p, AF.Copy)
-        Cu = su[2]
+            fill(sub(NG[1], IT, 16), 32768)
+            torow("Y", sub(NG[1], 0, IT), act(nhf, nh, AF.Copy), act(nlf, nl, AF.Copy))
+        if t == 1:
+            dma("Y", [old], [NG[2]], [(lambda: rows(NG[2], 0, 8), lambda: rows(NG[1], 0, 8))], 262144, nrows=16)
+        z2 = act(new("BB"), dab, AF.Relu, bias=131072.0, scale=-131072.0)
+        du = tt(new("FF"), mm(psum(), terms=[(IN if t else I1, z2), (F1, Cf)]), tO if t else tN, A.max if t else A.min)
+        du = ts(new("UU"), du, M - OFF if t else 0.0, None, A.add)
+        dma("G", [Q], [SF], [(lambda: rows(SF, 0, 8), lambda: rows(Q, 0, 8))], 131072, nrows=16)
+        if t < 2:
+            scatter("S", NS[t], du, SF, PAR["NCH"][t])
+        if t == 0:
+            at("M", 2)
+            pz = tolist(psum(), [(R412, Q)], [(IE, sn)], ch=128)
+            cond = tt(new("BB"), act(pz, pz, AF.Relu), rm, A.is_ge)
+        at("S", t)
+        sgather(S2, old, su[0])
+        tmp = new("FF")
+        for lo, n in chunks(128, PAR["LCH"][t]):
+            c = lambda r: sub(r, lo, n)
+            p, q = tolist(psum(n), [(R08, sub(S2, 16 * lo, 16 * n))]), psum(n)
+            tt(q, p, c(sf[0]), A.is_equal)
+            tt(c(tmp), q, c(D), A.mult)
+            tt(c(sf[1]), p, c(tmp), A.add)
+            ts(c(su[1]), c(sf[1]), -OFF, float(SENT), A.add, A.min)
+        at("T", t)
+        sgather(S3, old, su[1])
+        for lo, n in chunks(128, PAR["LCH"][t]):
+            c = lambda r: sub(r, lo, n)
+            p, q = tolist(psum(n), [(R08, sub(S3, 16 * lo, 16 * n))]), psum(n)
+            tt(c(e), p, c(hv), A.is_equal)
+            tt(q, p, c(sf[0]), A.is_equal)
+            tt(q, q, c(e), A.subtract)
+            tt(c(tmp), q, c(D), A.mult)
+            tt(c(sf[2]), p, c(tmp), A.add)
+            ts(c(su[2]), c(sf[2]), -OFF, float(SENT), A.add, A.min)
+        if t == 2:
+            at("N", t)
+            scatter("S", NS[2], du, SF, PAR["NCH"][2])
+        Cf, Cu = sf[2], su[2]
+        at("C", t)
         if t < 2:
             Cn = act(Cn, tt(Cn, Cn, Cf, A.min), bias=8192.0)
         else:
             ci = tt(new("II"), Cn, Cf, A.min)
             Cn = cp(Cn, ts(ci, ci, 8191, None, A.bitwise_and))
+        sg = [sub(sig, 0, 128), sub(sig, 128, 128)]
         for k in range(3):
+            at("XYZ"[k], t)
             pc = psum()
             for h in range(2):
                 l, u, o = reg("LT", k * M + 1024 * h, 1024), sub(su[k], 64 * h, 64), sub(pc, 64 * h, 64)
-                ex = [(I8, sub(sig, 128 * j + 64 * h, 64), False) for j in range(2 if k == 2 else 0)]
-                if 2 * k + h in XS[t]:
-                    sgather(l, XW, u)
+                ex = [(I8, sub(x, 64 * h, 64)) for x in (sg if k == 2 else [])]
+                if 2 * k + h in PAR["XS"][t]:
+                    sgather(l, XG, u)
                     for j in (0, 512):
-                        d = mm(psum(512), [(I1, sub(l, j, 512), False), (IN1, sub(K[t + 1], 1024 * h + j, 512), False)])
+                        d = mm(psum(512), terms=[(I1, sub(l, j, 512)), (IN, sub(K[t + 1], 1024 * h + j, 512))])
                         act(sub(l, j, 512), d, AF.Sign, bias=-0.5, scale=-1.0)
-                    mm(o, [(AH, l, True), (IN8, sub(CM1, 0, 64), False)] + ex)
+                    mm(o, [(AH, l)], [(I8, sub(fill(new("BB", 64), 1), 0, 64))] + ex)
                 else:
-                    vgather(l, XW, u, sub(K[t + 1], 1024 * h, 1024), A.is_lt)
-                    mm(o, [(ALL, l, True)] + ex)
+                    vgather(l, XG, u, sub(K[t + 1], 1024 * h, 1024), A.is_lt)
+                    mm(o, [(ALL, l)], ex)
             if k < 2:
-                act(sub(sig, 128 * k, 128), pc, AF.Sign, bias=-8.5)
+                act(sg[k], pc, AF.Sign, bias=-8.5)
+        at("E", t)
+        y3 = act(new("FF"), mm(psum(), terms=[(F1, sf[2]), (IZ, sg[0]), (IZ, sg[1])]), bias=6144.0 - OFF)
+        tt(y3, mm(psum(), terms=[(F1, sf[1]), (IZ, sg[0]), (IQ, sg[1]), (I1, C6K)]), y3, A.min)
+        tt(sub(T3, 0, 128), mm(psum(), terms=[(F1, sf[0]), (IE, sg[0]), (I1, C6K)]), y3, A.min)
         ts(has, pc, -7.5, None, A.is_gt)
-        pd = mm(psum(), [(I2, sub(sig, 0, 128), False), (I1, sub(sig, 128, 128), False)])
-        act(sub(T2, 0, 128), pd, AF.Relu, bias=1024.0, scale=-1024.0)
-        act(sub(T3, 0, 128), sub(T2, 0, 128), bias=8192.0)
         op("V", vc(128, 0.5), [has], [hs],
            lambda: g.vector.tensor_tensor_scan(ap(hs), ap(has), ap(has), 0.0, A.add, A.max), "scan")
-        pcum = mm(psum(), [(BD, hs, False)])
-        ppl = mm(psum(), [(BD, hs, False), (NUP, has, False)])
-        tt(sub(T1, 0, 128), ppl, has, A.mult)
-        nvs, colu = NVS[t], new("UU", 16)
-        if nvs:
-            ts(cb, pcum, 256.0, None, A.min)
-        for b in range(16):
-            jk, ac = reg("JK", 128 * b, 128), sub(acc, b, 1)
-            if b < nvs:
-                ts(jk, cb, sub(kb, b, 1), 0.5, A.is_lt, A.subtract)
-                op("V", vc(128, 1.0), [jk], [ac],
-                   lambda jk=jk, ac=ac: g.vector.tensor_reduce(ap(ac), ap(jk), AxisListType.X, A.add), "red")
+        nve = PAR["NVE"][t]
+        cv = mm(psum(8), terms=[(hs, GI)])
+        if nve < 8:
+            cs = act(new("FF", 8), mm(psum(8), terms=[(hs, GI)]), bias=0.5, scale=-1.0)
+        sd, rv = reg("SD", 272 * t, 272), reg("RV", 272 * t, 272)
+        nv = ts(sub(sd, 256, 16), sub(vv, 0, 16), mm(psum(1), terms=[(BD, sub(hs, 127, 1))]), 8192.0, A.is_ge, A.mult)
+        send(2 * t, nv, sub(rv, 256, 16))
+        for j in range(8):
+            if j < nve:
+                ts(sub(EE, 256 * j, 256), KI, sub(cv, j, 1), 2.0, A.is_ge, A.mult)
             else:
-                act(jk, pcum, AF.Sign, bias=sub(kb, b, 1), scale=-1.0, acc=ac)
-        for lo, n, s in ((0, nvs, 16.0), (nvs, 16 - nvs, 8.0)):
-            if n:
-                ts(sub(colu, lo, n), sub(acc, lo, n), s / 16.0, 64.0, A.mult, A.add)
-                act(sub(c16, lo, n), sub(acc, lo, n), bias=1024.0, scale=s)
+                act(sub(EE, 256 * j, 256), KI, AF.Sign, bias=sub(cs, j, 1))
+        tt(sub(T1, 0, 128), mm(psum(), terms=[(BD, hs), (NUP, has)]), has, A.mult)
+        pb = psum(16)
+        op("P", 0.06 + 1024 * PEC, [EE, ONE], [pb],
+           lambda pb=pb: [g.tensor.matmul(ap(sub(pb, b, 1)), T.EE[:, b::16], ap(sub(ONE, 0, 1)), True, True)
+                          for b in range(16)][-1], "mm")
+        colu = ts(new("UU", 16), pb, offe[nve], 0.5, A.add, A.mult)
         vgather(G1, T1, colu, X1, A.is_equal)
         vgather(G2, T3, colu, G1, A.mult)
-        pw = tolist(psum(16), [(RA, G1), (ALL, G2)], [(I1, c16)])
-        sd = reg("SD", 272 * t, 272)
-        offu = ts(new("UU", 16), pw, -8192.0, 0.0, A.add, A.max)
-        nv = ts(sub(sd, 256, 16), pw, 8000.0, 8192.0, A.is_lt, A.mult)
-        sgather(ER, reg("SR", 3 * t * M, 3 * M), offu)
-        pe = tolist(psum(16), [(R08, ER)])
-        sgather(sub(sd, 0, 256), XW, cp(new("UU", 16), pe))
-        tt(em, pe, nv, A.add)
-        rv, link = reg("RV%d" % t, 0, 272), ("link", t, t + 1, None)
-        op("G", 1.0, [sd], [link],
-           lambda t=t, sd=sd, rv=rv: g.remote_dma(ap(rv), ap(sd), T.sem["rv%d" % t], T.sem["sn%d" % t], peer[1], peer[0], peer[2]),
-           "send", lat=0.0, kind="r")
-        op(None, 0.0, [link], [rv], None, "recv", lat=2.5, kind="rv%d" % t)
-        tt(e3, em, sub(rv, 256, 16), A.add)
-        tt(e3, e3, tX, A.min)
-        scatter("V", XW, cp(new("UU", 16), e3), sub(rv, 0, 256))
-    dma("Y", [K[3]], [], [(lambda: T.yk[:], lambda: ap(K[3]))], 524288)
-    dma("Y", [Cn], [], [(lambda: T.yc[:], lambda: ap(Cn))], 65536)
-    yn = ("yn", 0, 1, None)
-    dma("G", [NWIN], [yn], [(lambda: T.yn[:], lambda: rows(NLO, 0, 16))], 131072, nrows=16)
-    dma("G", [NWIN], [yn], [(lambda h=h: T.yn[:, h:h + M], lambda h=h: rows(sub(NLO, h, M), 8, 16)) for h in (0, M)],
-        131072, nrows=16, accum_op=A.add)
-    dma("Y", [XW], [], [(lambda: T.yx[:], lambda: T.XX[:, 0:IT])], 1048576)
+        pe = mm(psum(16), [(ALH, G2)])
+        sgather(sub(sd, 0, 256), XG, ts(new("UU", 16), pe, 2048.0, None, A.add))
+        send(2 * t + 1, sub(sd, 0, 256), sub(rv, 0, 256))
+        ef = act(new("FF", 16), pe, bias=2048.0)
+        pd = mm(psum(16), terms=[(F1, ef), (I1, nv), (I1, sub(rv, 256, 16))])
+        scatter("V", XS_, cp(new("UU", 16), tt(new("FF", 16), pd, tX, A.min)), sub(rv, 0, 256), 256)
+    at("O", 0)
+    none = act(new("BB"), sf[0], AF.Relu, bias=-2048.0 * (OFF + IT - 1), scale=2048.0)
+    sgather(GL, KWIN[3], ts(new("UU"), mm(psum(), terms=[(F1, vv), (I1, none)]), float(M), None, A.min))
+    dma("S", [GL], [], [(lambda: T.yk[:], lambda: ap(GL))], 524288)
+    dma("S", [Cn], [], [(lambda: T.yc[:], lambda: ap(Cn))], 65536)
+    NE = sub(NG[2], 0, IT)
+    dma("Y", [NE], [nhf, nlf], [(lambda: ap(nhf), lambda: rows(NE, 0, 16)), (lambda: ap(nlf), lambda: rows(NE, 8, 16))],
+        262144, nrows=256)
+    ne = cp(nhf, ts(nx, mm(psum(256), terms=[(F1, nhf), (F1, nlf)]), -OFF, None, A.add))
+    dma("S", [ne], [], [(lambda: T.yn[:], lambda: ap(ne))], 131072)
+    dma("Y", [XS_], [], [(lambda: T.yx[:], lambda: T.XX[:, 0:IT])], 1048576)
     return ops, bank
 
 
@@ -460,7 +600,7 @@ def deal(ops, seq, eng):
     while rest:
         for i, k in enumerate(rest):
             o = ops[k]
-            if all(j in pos for j in o["dep"]) and (all(v in bank for v in o["pv"]) or None in holder):
+            if all(j in pos for j in o["dep"]) and sum(v not in bank for v in o["pv"]) <= holder.count(None):
                 break
         else:
             return None
@@ -475,31 +615,33 @@ def deal(ops, seq, eng):
             if last[b] >= 0 and (fresh or eng[last[b]] != eng[k]):
                 d.add(last[b])
             last[b] = k
+        for v in o["pv"]:
             left[v] -= 1
             if left[v] == 0:
-                holder[b] = None
+                holder[bank[v]] = None
         pos[k] = len(order)
         order.append(k)
         dep[k] = d
     return order, bank, dep
 
 
-def length(ops, order, dep, eng, m):
-    free, fin = {}, {}
-    for k in order:
-        o = ops[k]
-        d = o["dur"] * m.get(o["name"], m["c"] if o["eng"] in ("V", "S") else 1.0)
-        o["start"] = s = max([fin[j] for j in dep[k]] + [free.get(eng[k], 0.0)])
-        fin[k] = s + d + o["lat"] * (m["lat"] if o["kind"] == "c" else 1.0)
-        if o["eng"]:
-            free[eng[k]] = s + d
-    return max(fin.values())
+def costs(ops, m):
+    gather, scatter, tensor, other, fixed, wake, dma, remote = m
+    dur, lat = [], []
+    for o in ops:
+        d, f, name = o["dur"], 0.06, o["name"]
+        if o["kind"] == "c":
+            r = {"sg": gather, "vg": gather, "sc": scatter, "mm": tensor}.get(name, other)
+            d = (d - f) * r + (f if name in ("sg", "vg", "sc", "iota") else f * fixed)
+        dur.append(d * remote / 2.5 if o["eng"] == "G" and o["kind"] != "c" else d)
+        lat.append({"c": wake, "m": o["lat"] + dma, "d": 0.0, "r": 0.0}.get(o["kind"], remote - 0.4))
+    return dur, lat
 
 
-COSTS = [{"sg": a, "vg": a, "sc": b, "mm": c, "lat": d, "c": e} for a, b, c, d, e in
-         ((0.7, 0.5, 1.0, 1.0, 0.85), (1.3, 1.5, 1.0, 1.0, 1.1), (0.7, 1.5, 1.5, 2.0, 1.0), (1.3, 0.5, 0.7, 0.5, 1.0),
-          (0.8, 0.8, 1.7, 1.0, 0.8), (1.0, 1.0, 1.0, 1.0, 1.0))]
-WEIGHT = (110.0, 180.0, 160.0, 140.0, 130.0, 60.0)
+COSTS = ((0.72, 0.6, 1.25, 1.15, 0.6, 0.15, 1.6, 3.2), (1.45, 1.8, 1.15, 1.15, 0.5, 0.1, 1.5, 2.5),
+         (0.75, 1.3, 0.9, 0.9, 0.7, 0.15, 2.0, 3.0), (1.2, 0.6, 1.2, 1.1, 0.5, 0.12, 1.4, 2.6),
+         (0.88, 0.88, 1.0, 1.0, 0.6, 0.14, 1.5, 2.8))
+WEIGHT = (80.0, 160.0, 120.0, 115.0, 60.0)
 
 
 def schedule(ops):
@@ -509,45 +651,199 @@ def schedule(ops):
         for j in pred[k]:
             succ[j].append(k)
     eng, dur, lat, zero = [o["eng"] for o in ops], [o["dur"] for o in ops], [o["lat"] for o in ops], [0.0] * n
+    anc, near = [0] * n, []
+    for k in range(n):
+        far = 0
+        for j in pred[k]:
+            far |= anc[j]
+        near.append([j for j in pred[k] if not far >> j & 1])
+        anc[k] = far | sum(1 << j for j in pred[k])
+    steps = [o["step"] for o in ops]
+    after = [[] for _ in ops]
+    for k in range(n):
+        for j in near[k]:
+            after[j].append(k)
 
-    def run(key, eng):
-        for k in range(n):
-            for j in pred[k]:
-                if key[k] < key[j]:
-                    key[k] = key[j]
-        st, fin = place(sorted(range(n), key=lambda k: (key[k], k)), pred, eng, dur, zero, lat)
-        bs, bf = place(sorted(range(n), key=lambda k: (-fin[k], -k)), succ, eng, dur, lat, zero)
-        st, fin = place(sorted(range(n), key=lambda k: (-bf[k], k)), pred, eng, dur, zero, lat)
-        return max(fin), st
+    either = ["alt" in o for o in ops]
 
-    rng = np.random.RandomState(SEED)
-    cur, st = run([float(k) for k in range(n)], eng)
-    best, low, flex = None, cur, [k for k in range(n) if "alt" in ops[k]]
-    for it in range(TRIES):
-        key = list(st)
-        for _ in range(rng.randint(0, 3)):
-            a, w, d = rng.randint(n), rng.randint(1, 40), float(rng.randn()) * 8.0
-            for k in range(a, min(n, a + w)):
-                key[k] += d
-        e2 = list(eng)
-        if rng.rand() < 0.3:
+    def first(due, shift=zero):
+        key, eng = [0.0] * n, [o["eng"] for o in ops]
+        for k in reversed(range(n)):
+            key[k] = min([due[steps[k]]] + [key[j] for j in after[k]]) - dur[k] - lat[k] + shift[k]
+        wait, ready, free, order = [len(p) for p in near], [0.0] * n, {e: 0.0 for e in eng}, []
+        left, bank, idle, last = dict(uses), {}, list(range(8)), [0.0] * 8
+        can = [k for k in range(n) if not wait[k]]
+        while can:
+            low, cand = 1e9, []
+            for k in can:
+                s = max(ready[k], free[eng[k]])
+                need = 0
+                for v in pvs[k]:
+                    if v in bank:
+                        s = max(s, last[bank[v]])
+                    else:
+                        need += 1
+                if need:
+                    if need + spare[k] > len(idle):
+                        continue
+                    s = max(s, last[idle[0]])
+                cand.append((key[k], k, s, eng[k]))
+                if s + dur[k] < low:
+                    low, e = s + dur[k], eng[k]
+                if either[k]:
+                    s2 = max(ready[k], free["V"])
+                    if s2 < s - due["gap"]:
+                        cand.append((key[k] + due["bias"], k, s2, "V"))
+                        if s2 + dur[k] < low:
+                            low, e = s2 + dur[k], "V"
+            if not cand:
+                return None
+            cand = [c for c in cand if c[3] == e]
+            soon = min(c[2] for c in cand)
+            soon += PAR["LOOK"] * (low - soon)
+            k, s = min(c for c in cand if c[2] <= soon)[1:3]
+            eng[k] = e
+            can.remove(k)
+            order.append(k)
+            if e:
+                free[e] = s + dur[k]
+            f = s + dur[k] + lat[k]
+            for v in pvs[k]:
+                if v not in bank:
+                    bank[v] = idle.pop(0)
+                last[bank[v]] = f
+                left[v] -= 1
+                if not left[v]:
+                    idle.append(bank[v])
+            for j in after[k]:
+                ready[j] = max(ready[j], f)
+                wait[j] -= 1
+                if not wait[j]:
+                    can.append(j)
+        return order, eng
+
+    durs, lats = zip(*[costs(ops, m) for m in COSTS])
+    dur, lat = durs[-1], lats[-1]
+    pvs = [o["pv"] for o in ops]
+    uses = {}
+    for p in pvs:
+        for v in p:
+            uses[v] = uses.get(v, 0) + 1
+    spare = [1 if len(p) == 1 else 0 for p in pvs]
+
+    marks = [max(k for k in range(n) if steps[k] == s) for s in PAR["MARK"].split()]
+    timed = [[k - 1] if ops[k]["kind"] == "m" else near[k] for k in range(n)]
+
+    def judge(order, eng, same=0, old=None):
+        left, bank, free, last, dep, qp, at = dict(uses), {}, list(range(8)), [-1] * 8, list(timed), [-1] * n, {}
+        for k in order:
+            e = eng[k]
+            if e:
+                qp[k] = at.get(e, -1)
+                at[e] = k
+            for v in pvs[k]:
+                b = bank.get(v)
+                if b is None:
+                    if not free:
+                        return None
+                    b = bank[v] = free.pop(0)
+                    if last[b] >= 0:
+                        dep[k] = dep[k] + [last[b]]
+                elif eng[last[b]] != e:
+                    dep[k] = dep[k] + [last[b]]
+                last[b] = k
+            for v in pvs[k]:
+                left[v] -= 1
+                if not left[v]:
+                    free.append(bank[v])
+        sc, out, rest = 0.0, [], order[same:]
+        for m, (du, la, w) in enumerate(zip(durs, lats, WEIGHT)):
+            fin, end = (list(old[m][0]), list(old[m][1])) if same else ([0.0] * n, [0.0] * (n + 1))
+            for k in rest:
+                s = end[qp[k]]
+                for j in dep[k]:
+                    if fin[j] > s:
+                        s = fin[j]
+                s += du[k]
+                end[k] = s
+                fin[k] = s + la[k]
+            sc += (max(fin) + PAR["PULL"] * sum(fin[k] for k in marks)) / w
+            out.append((fin, end))
+        return sc, out, dep, qp, bank
+
+    rng = np.random.RandomState(PAR["SEED"])
+    due = dict(PAR["DUE"])
+    names = sorted(due)
+    order, eng = first(due)
+    now = judge(order, eng)
+    for it in range(PAR["ROUGH"]):
+        d2 = dict(due)
+        for _ in range(rng.randint(1, 3)):
+            x = names[rng.randint(len(names))]
+            d2[x] += float(rng.randn()) * (0.5 if x == "gap" else 3.0)
+        o2 = first(d2)
+        got = o2 and judge(*o2)
+        if got and got[0] < now[0] + PAR["MIDT"] * (1.0 - it / PAR["ROUGH"]) * rng.rand():
+            now, order, eng, due = got, o2[0], o2[1], d2
+    FOUND_DUE.append(due)
+
+    def critical(now, m):
+        (fin, end), dep, qp = now[1][m], now[2], now[3]
+        k, arcs, flex = marks[rng.randint(len(marks))] if rng.rand() < 0.4 else fin.index(max(fin)), [], []
+        while k >= 0:
+            s, j = end[k] - durs[m][k], -1
+            for i in dep[k]:
+                if fin[i] > s - 1e-9:
+                    j = i
+            if j < 0 and qp[k] >= 0 and end[qp[k]] > s - 1e-9:
+                j = qp[k]
+            if j >= 0 and not anc[k] >> j & 1:
+                arcs.append((j, k))
+            if "alt" in ops[k]:
+                flex.append(k)
+            k = j
+        return arcs, flex
+
+    best, tries = (now[0], order, eng), PAR["TRIES"]
+    for it in range(tries):
+        arcs, flex = critical(now, rng.randint(len(COSTS)))
+        qp = now[3]
+        o2, e2 = order, eng
+        if flex and rng.rand() < PAR["FLIP"][1]:
             k = flex[rng.randint(len(flex))]
+            e2 = list(eng)
             e2[k] = "V" if e2[k] == "S" else "S"
-        m, s2 = run(key, e2)
-        if m < cur or rng.rand() < np.exp((cur - m) / (TEMP * (1.0 - it / TRIES) + 0.02)):
-            cur, st, eng = m, s2, e2
-            if m < low + 1.0 or best is None:
-                low = min(low, m)
-                got = deal(ops, sorted(range(n), key=lambda k: (st[k], k)), eng)
-                if got:
-                    ls = [length(ops, got[0], got[2], eng, c) for c in COSTS]
-                    sc = sum(x / w for x, w in zip(ls, WEIGHT))
-                    if best is None or sc < best[0]:
-                        best = (sc, got + (eng,), ls)
-    return best
+            a = order.index(k)
+        elif not arcs:
+            continue
+        else:
+            j, k = arcs[rng.randint(len(arcs))]
+            ahead = rng.rand() < 0.5
+            while ahead and rng.rand() < 0.5 and qp[j] >= 0 and not anc[k] >> qp[j] & 1:
+                j = qp[j]
+            a, b = order.index(j), order.index(k) + 1
+            if not ahead:
+                b = min(n, b + rng.randint(0, 2) * rng.randint(0, 30))
+            seg = order[a:b]
+            if ahead:
+                front = [x for x in seg if x == k or anc[k] >> x & 1]
+                back = [x for x in seg if not (x == k or anc[k] >> x & 1)]
+            else:
+                front = [x for x in seg if not (x == j or anc[x] >> j & 1)]
+                back = [x for x in seg if x == j or anc[x] >> j & 1]
+            o2 = order[:a] + front + back + order[b:]
+        got = judge(o2, e2, a, now[1])
+        if got and (got[0] < now[0] or rng.rand() < np.exp((now[0] - got[0]) / (PAR["TEMP"] * (1.0 - it / tries) + 1e-4))):
+            now, order, eng = got, o2, e2
+            if now[0] < best[0]:
+                best = (now[0], order, eng)
+    got = judge(best[1], best[2])
+    dep = {k: set(pred[k]) | set(got[2][k]) for k in range(n)}
+    return best[0], (best[1], got[4], dep, best[2]), [max(f) for f, e in got[1]]
 
 
 FOUND = []
+FOUND_DUE = []
 
 
 def rank_program(g, core, T, topo):
@@ -575,12 +871,17 @@ def rank_program(g, core, T, topo):
     nd, final = 0, {}
     for k in order:
         o = ops[k]
-        if o["eng"] is None:
+        if o["name"] == "recv":
             o["tok"], o["clock"] = (o["kind"], n_in), {}
             final[o["kind"]] = n_in
             continue
+        if o["kind"] == "m":
+            o["tok"], o["clock"] = ops[k - 1]["tok"], ops[k - 1]["clock"]
+            continue
         kn = known[o["eng"]]
         for j in sorted(dep[k], key=lambda j: -pos[j]):
+            if ops[j]["kind"] == "d":
+                continue
             s, v = ops[j]["tok"]
             if kn.get(s, 0) < v:
                 queue[o["eng"]].wait_ge(T.sem[s], v)
@@ -601,7 +902,7 @@ def rank_program(g, core, T, topo):
         else:
             continue
         final[o["tok"][0]] = o["tok"][1]
-    for t in range(RO):
+    for t in range(2 * RO):
         final["sn%d" % t] = n_out
     for s, v in final.items():
         g.sync.wait_ge(T.sem[s], v)

import numpy as np
from concourse.mybir import AluOpType, ActivationFunctionType

A = AluOpType
AF = ActivationFunctionType
IT, M, RO = 4096, 2048, 3
OFF = 16384.0
SENT = IT
KW, GW = M + 16, IT + 16
NW, XW = GW + M, GW + 256

SCRATCH = {"KK": 4 * KW, "XX": XW, "NN": GW, "GL": M, "LE": M, "LT": 3 * M, "PP": M, "ZR": M, "QQ": M, "SR": 2 * M,
           "SB": M, "W0": 4 * M, "EE": M, "SD": 3 * 272, "RV": 3 * 272, "BB": 80 * 128}
SCRATCH = {k: ("sbuf", [128, n], "bfloat16") for k, n in SCRATCH.items()}
SCRATCH.update({k: ("sbuf", [128, n], "float32") for k, n in (("SF", M), ("NF", NW + GW), ("FF", 90 * 128))})
SCRATCH.update({"II": ("sbuf", [128, 12 * 128], "int32"), "UU": ("sbuf", [128, 30 * 128], "uint16"),
                "HH": ("sbuf", [128, 512], "float16")})
SCRATCH.update({"PS%d" % k: ("psum", [128, 512], "float32") for k in range(8)})
SEMAPHORES = ["cV", "cS", "cP", "cG"] + ["d%d" % k for k in range(44)] + [s + str(k) for s in ("rv", "sn") for k in range(2 * RO)]

PAR = {"XS": ((), (), (1,)),
       "NVE": (4, 4, 5),
       "DCH": (64, 128, 128),
       "LCH": (64, 128, 128),
       "CLR": "VVVVVSSS VVVV SSGG",
       "NMS": 4096,
       "VCH": 1024, "GCH": 1024, "SCH": 512, "NCH": (512, 512, 512),
       "TWO": (0,),
       "DUE": dict([(s + str(t), d) for s, ds in (("M", (10, 24, 46)), ("K", (15, 38, 60)), ("W", (18, 36, 56)),
                                                  ("P", (12, 40, 61)), ("Q", (21, 43, 64)), ("S", (27, 47, 68)),
                                                  ("T", (32, 51, 72)), ("X", (26, 48, 72)), ("Y", (31, 52, 75)),
                                                  ("Z", (36, 56, 78)), ("E", (45, 66, 89)), ("N", (38, 54, 90)),
                                                  ("C", (90, 90, 90))) for t, d in enumerate(ds)]
                   + [("O0", 95), ("A", 95), ("H0", 7), ("H1", 8), ("gap", 0.5), ("bias", 3.0)]),
       "MERGE": False, "MARK": "W0 E0 Q1 E1 Q2 Z2", "PULL": 0.07, "MIDT": 0.01, "FLIP": (0.0, 0.05, 0.1), "LOOK": 0.5, "ROUGH": 1500, "SEED": 5, "TRIES": 38000, "TEMP": 0.01}
CY, GA, SC, PEC, LAT = 1.0e-3, 1.3, 3.0, 0.52e-3, 0.12
SIZE = {"float32": 4, "int32": 4, "bfloat16": 2, "uint16": 2, "float16": 2}


def plan(T, g, peer):
    ops, bank, npv, step = [], {}, [0], ["A"]
    top = {"FF": 0, "BB": 0, "II": 0, "UU": 0, "HH": 0}
    GCH = PAR["GCH"]

    def new(b, n=128):
        lo = top[b]
        top[b] = lo + (n + 15) // 16 * 16
        assert top[b] <= SCRATCH[b][1][1], b
        return (b, lo, lo + n, None)

    def reg(b, lo, n):
        return (b, lo, lo + n, None)

    def sub(r, lo, n, tag=None):
        return (r[0], r[1] + lo, r[1] + lo + n, tag)

    def psum(n=128):
        npv[0] += 1
        return (("ps", npv[0]), 0, n, None)

    def isps(r):
        return isinstance(r[0], tuple)

    def size(r):
        return 4 if isps(r) else SIZE[SCRATCH[r[0]][2]]

    def ap(r):
        return T["PS%d" % bank[r[0]] if isps(r) else r[0]][:, r[1]:r[2]]

    def rows(r, first, step):
        return T[r[0]][first::step, r[1]:r[2]]

    def val(s):
        return ap(s) if isinstance(s, tuple) else s

    def op(eng, dur, rd, wr, fn, name, lat=LAT, inc=1, kind="c"):
        ops.append({"eng": eng, "dur": dur, "rd": rd, "wr": wr, "fn": fn, "lat": lat, "inc": inc, "kind": kind, "name": name,
                    "step": step[0]})

    def at(name, t):
        step[0] = name + str(t)

    def vc(n, f):
        return 0.05 + max(64, n * f) * CY

    def half(*rs):
        return 0.5 if all(size(r) == 2 for r in rs) else 1.0

    def ts(o, i, s1, s2, o0, o1=None):
        rd = [i] + [s for s in (s1, s2) if isinstance(s, tuple)]
        if o1 is None:
            f = lambda: g.vector.tensor_scalar(ap(o), ap(i), val(s1), None, o0)
        else:
            f = lambda: g.vector.tensor_scalar(ap(o), ap(i), val(s1), val(s2), o0, o1)
        op("V", vc(i[2] - i[1], half(o, i)), rd, [o], f, "ts")
        return o

    def tt(o, a, b, o0):
        f = half(o, a, b) * (1 if isps(a) or isps(b) else 2)
        op("V", vc(a[2] - a[1], f), [a, b], [o], lambda: g.vector.tensor_tensor(ap(o), ap(a), ap(b), o0), "tt")
        return o

    def cp(o, i):
        op("V", vc(i[2] - i[1], half(o, i)), [i], [o], lambda: g.vector.tensor_copy(ap(o), ap(i)), "cp")
        return o

    def ms(o, c):
        op("V", vc(o[2] - o[1], half(o)), [], [o], lambda: g.vector.memset(ap(o), float(c)), "ms")
        return o

    def act(o, i, fn=AF.Identity, bias=0.0, scale=1.0):
        rd = [i] + [s for s in (bias, scale) if isinstance(s, tuple)]
        op("S", 0.07 + max(64, i[2] - i[1]) * CY, rd, [o],
           lambda: g.scalar.activation(ap(o), ap(i), fn, bias=val(bias), scale=val(scale)), "act")
        return o

    def iota(o, pat, base, cm):
        if o[0] != "II":
            f = lambda: g.iota(ap(o), pat, base, cm, allow_small_or_imprecise_dtypes=True)
        else:
            f = lambda: g.iota(ap(o), pat, base, cm)
        op("G", 0.13 + 2 * (o[2] - o[1]) * CY, [], [o], f, "iota")
        return o

    def fill(o, c):
        return iota(o, [[0, o[2] - o[1]]], c, 0)

    def keep(o, i, pat, how, c, base, cm):
        op("G", 0.17 + 2 * (o[2] - o[1]) * CY, [i], [o],
           lambda: g.affine_select(ap(o), ap(i), pat, how, float(c), base, cm), "iota")
        return o

    def chunks(n, c):
        return [(lo, min(c, n - lo)) for lo in range(0, n, c)]

    def sgather(o, win, off):
        for lo, n in chunks(o[2] - o[1], GCH):
            oo, ff = sub(o, lo, n), sub(off, lo // 16, n // 16)
            op("S", 0.065 + n * GA * CY, [win, ff], [oo],
               lambda oo=oo, ff=ff: g.scalar.activation(ap(oo), ap(win).indirect(ap(ff)), AF.Copy), "sg")
            ops[-1]["alt"] = lambda oo=oo, ff=ff: g.vector.tensor_copy(ap(oo), ap(win).indirect(ap(ff)))

    def vgather(o, win, off, in1, o0):
        for lo, n in chunks(o[2] - o[1], PAR["VCH"]):
            oo, ff, i1 = sub(o, lo, n), sub(off, lo // 16, n // 16), sub(in1, lo, n)
            op("V", 0.05 + n * GA * CY, [win, ff, i1], [oo],
               lambda oo=oo, ff=ff, i1=i1: g.vector.tensor_tensor(ap(oo), ap(win).indirect(ap(ff)), ap(i1), o0), "vg")

    def scatter(eng, win, off, src, ch):
        for lo, n in chunks(src[2] - src[1], ch):
            ss, ff = sub(src, lo, n), sub(off, lo // 16, n // 16)
            f = fv = lambda ss=ss, ff=ff: g.vector.tensor_copy(ap(win).indirect(ap(ff)), ap(ss))
            if eng == "S":
                f = lambda ss=ss, ff=ff: g.scalar.activation(ap(win).indirect(ap(ff)), ap(ss), AF.Silu)
            op(eng, 0.06 + n * SC * CY, [ss, ff], [win], f, "sc")
            if eng == "S":
                ops[-1]["alt"] = fv

    def mm(o, lists=(), terms=()):
        n = max(64, o[2] - o[1])
        cyc = 16 * n * len(lists) + sum(n * (4 if size(r) == 4 else 1) for l, r in terms)

        def f():
            pairs = []
            for l, r in lists:
                pairs += [(T[l[0]][:, l[1] + 16 - i:l[1] + 144 - i], T[r[0]][:, r[1] + i:r[2]:16]) for i in range(16)]
            pairs += [(ap(l), ap(r)) for l, r in terms]
            return [g.tensor.matmul(ap(o), l, r, k == 0, k == len(pairs) - 1) for k, (l, r) in enumerate(pairs)][-1]
        op("P", 0.06 + cyc * PEC, [x for p in list(lists) + list(terms) for x in p], [o], f, "mm")
        return o

    def tolist(o, lists, terms=(), ch=64):
        for lo, n in chunks(o[2] - o[1], ch):
            mm(sub(o, lo, n), [(s, sub(tab, 16 * lo, 16 * n)) for s, tab in lists], [(l, sub(r, lo, n)) for l, r in terms])
        return o

    def dma(q, rd, wr, pairs, nbytes, nrows=128, after=(), turn=False):
        e = {"Y": g.sync, "S": g.scalar, "G": g}[q]
        link, done = ("dma", len(ops), len(ops) + 1, None), ("done", len(ops), len(ops) + 1, None)
        op(q, {"Y": 0.2, "S": 0.15, "G": 1.6}[q] * len(pairs), rd + list(after), wr + [link] + [("turn" + q, 0, 1, None)] * turn,
           lambda: [e.dma_start(o(), i()) for o, i in pairs], "dma", inc=16 * len(pairs), kind="d")
        op("D", nbytes / 320e3 + nrows * 0.0015, rd + [link], wr + [done] + [("turn", 0, 1, None)] * turn, None, "move",
           lat=0.5 if q == "G" else 0.0, kind="m")
        return done

    def load(q, name, r, nbytes=65536, after=()):
        dma(q, [], [r], [(lambda: ap(r), lambda: T[name][:])], nbytes, after=after, turn=not after)
        return r

    def torow(q, tab, hi, lo):
        return dma(q, [hi, lo], [tab], [(lambda: rows(tab, 0, 16), lambda: ap(hi)), (lambda: rows(tab, 8, 16), lambda: ap(lo))],
                   65536, nrows=256)

    def copy(o, i):
        return dma("Y", [i], [o], [(lambda: ap(o), lambda: ap(i))], 524288)

    def send(k, src, dst):
        link = ("link", k, k + 1, None)
        op("G", 1.0, [src], [link],
           lambda: g.remote_dma(ap(dst), ap(src), T.sem["rv%d" % k], T.sem["sn%d" % k], peer[1], peer[0], peer[2]),
           "send", lat=0.0, kind="r")
        op("D", 0.2 + 0.2 * (k % 2), [link], [dst], None, "recv", lat=2.5, kind="rv%d" % k)

    K = [reg("KK", t * KW, M) for t in range(4)]
    KWIN = [reg("KK", t * KW, KW) for t in range(4)]
    kl = load("Y", "kl", new("II"))
    kr = load("S", "kr", new("II"))
    nx = load("S", "nxt", new("II", 256), 131072)
    load("Y", "ky", K[0], 524288)
    tgt, par, siz, cur = [load("Y", n, new("II")) for n in ("tgt", "par", "siz", "cur")]
    XG, XS_, NLO = reg("XX", 0, GW), reg("XX", 0, XW), reg("NN", 0, IT)
    NG = [reg("NN", 0, GW), reg("NF", 0, GW), reg("NF", NW, GW)]
    NS = [reg("NF", 0, NW), reg("NF", GW, NW), reg("NF", GW, NW)]

    X1 = iota(new("FF", 256), [[1, 256]], 1, 0)
    pi = iota(new("II", 1), [[0, 1]], 0, 1)
    pf = iota(new("FF", 1), [[0, 1]], 0, 1)
    for t in range(4):
        fill(reg("KK", t * KW + M, 16), 255)
    ZERO, ONE = fill(new("FF", 144), 0), fill(new("BB", 144), 1)
    vp = iota(new("FF"), [[16, 128]], 0, 1)

    def diag(o, c):
        return keep(o, sub(ZERO, 0, 128), [[-1, 128]], A.not_equal, c, 0, 1)

    def picks(rs, c):
        o = new("BB", 144)
        for k, r in enumerate(rs):
            keep(o, o if k else ZERO, [[-16, 9], [-256, 16]], A.not_equal, c, 16 - r, 1)
        return o

    ALL = keep(new("BB", 144), ONE, [[-16, 9], [-256, 16]], A.is_ge, 0.0, 16, 1)
    keep(ALL, ALL, [[16, 9], [0, 16]], A.is_ge, 0.0, -1, -1)
    R4, R08, R412 = picks((4,), 1.0), picks((0, 8), 1.0), picks((4, 12), 1.0)
    I1, IN, IK, IZ, IQ, I8, IE, IG, IX = [diag(new("BB"), s) for s in
                                          (1.0, -1.0, 2048.0, 4096.0, -4096.0, 8.0, -8192.0, 2.0 ** 24, -32768.0)]
    F1, FN = diag(new("FF"), 1.0), diag(new("FF"), -1.0)
    dh, dl = iota(new("BB"), [[0, 128]], 128 * 128, 128), iota(new("BB"), [[1, 128]], 128, 0)
    C6K = fill(new("BB"), 6144 - int(OFF))
    KI = iota(new("BB", 256), [[1, 16], [16, 16]], 0, 0)
    BD = keep(new("BB"), sub(ONE, 0, 128), [[-16, 8], [0, 16]], A.is_ge, 0.0, 0, 1)
    keep(BD, BD, [[16, 8], [0, 16]], A.is_ge, 0.0, 15, -1)
    NUP = fill(new("BB"), -1)
    keep(NUP, NUP, [[16, 8], [0, 16]], A.is_ge, 0.0, 15, -1)
    keep(NUP, NUP, [[-1, 128]], A.is_ge, 0.0, -1, 1)
    GI = keep(new("BB", 8), sub(ONE, 0, 8), [[-16, 8]], A.is_ge, 0.0, 0, 1)
    keep(GI, GI, [[16, 8]], A.is_ge, 0.0, 15, -1)
    offe = {n: keep(o, fill(o, 128), [[0, 1]], A.is_ge, 0.0, -16 * n, 1) for n in sorted(set(PAR["NVE"])) for o in [new("FF", 1)]}
    ALH = cp(new("HH", 144), ALL)
    ng = tt(new("FF", 1), ts(new("II", 1), pi, 15, None, A.bitwise_and), pf, A.subtract)
    vv = act(new("FF"), vp, bias=ng)
    tN = act(new("FF"), vv, bias=float(GW))
    tO = act(new("FF"), vv, bias=OFF - M)
    tX = sub(tN, 0, 16)
    cq = act(new("FF", 1), ng, bias=-16512.0, scale=128.0)
    cG = act(new("FF"), vv, bias=cq, scale=-1.0)
    if any(PAR["XS"]):
        AH = act(new("BB", 144), ALL, scale=0.5)
    SB, SF = reg("SB", 0, M), reg("SF", 0, M)
    W = [reg("W0", 0, 3 * M), reg("W0", 0, 4 * M)]
    WA, WB = reg("W0", 2 * M, M), reg("W0", 3 * M, M)
    for tab, way in zip((NLO, SB, WA), PAR["CLR"].split()):
        for k, e in enumerate(way):
            o = sub(tab, 512 * k, 512)
            fill(o, 0) if e == "G" else ms(o, 0) if e == "V" else act(o, reg("NN", 0, 512), AF.Copy)
    at("H", 1)
    torow("Y", SB, dh, dl)
    wa = torow("Y", WA, dh, dl)
    at("A", "")
    fill(reg("NN", IT, 16), 32768)
    fill(reg("XX", IT, 16), 255)
    T1, T3 = new("FF", 144), new("FF", 144)
    fill(sub(T1, 128, 16), 0)
    fill(sub(T3, 128, 16), 0)

    nh = ts(new("BB", 256), nx, OFF - 192.0, None, A.add)
    nl = act(new("BB", 256), tt(new("FF", 256), nx, nh, A.subtract), bias=OFF)
    nhf, nlf = new("FF", 256), new("FF", 256)
    at("H", 0)
    na = torow("Y", NLO, nh, nl)
    at("A", "")
    load("Y", "x", reg("XX", 0, IT), 1048576, after=[na, wa])
    zh = cp(new("BB"), siz)
    zl = tt(new("BB"), siz, zh, A.subtract)
    zp = psum(256)
    mm(sub(zp, 0, 128), terms=[(zh, I1)])
    mm(sub(zp, 128, 128), terms=[(zl, I1)])
    zt = act(new("BB", 256), zp, AF.Copy)
    ZR = reg("ZR", 0, M)
    dma("Y", [zt], [ZR], [(lambda k=k: T.ZR[16 * (k % 8) + 4 + 8 * (k // 8):16 * (k % 8) + 5 + 8 * (k // 8), :],
                           lambda k=k: ap(sub(zt, 16 * k, 16))) for k in range(16)], 65536, nrows=1024)
    for lo in range(0, M, 512):
        fill(sub(SF, lo, 512), 0)
        if PAR["MERGE"]:
            fill(sub(WB, lo, 512), 0)
    if PAR["MERGE"]:
        torow("Y", WB, dh, dl)
    for tab in NG[1:]:
        for lo, n in chunks(GW, 688):
            fill(sub(tab, lo, n), 0)

    klu, kru = cp(new("UU"), kl), cp(new("UU"), kr)
    cV, kh = ts(new("FF"), kl, 2.0 * M, None, A.add), new("FF", 256)
    tt(sub(kh, 0, 128), kr, kl, A.subtract)
    kv = tt(sub(kh, 128, 128), vv, cV, A.subtract)
    T1p = tt(new("FF"), tgt, par, A.mult)
    T0p = tt(new("FF"), tgt, T1p, A.subtract)
    room = tt(new("FF"), T0p, siz, A.subtract)
    par0 = ts(new("BB"), par, -1.0, 1.0, A.mult, A.add)
    nwl = [ts(new("BB"), room, 0.5, 64.0, A.is_lt, A.mult), tt(new("BB"), siz, T1p, A.is_ge)]
    nwd = [None, act(new("BB"), T1p, AF.Relu, bias=64.0, scale=-64.0), act(new("BB"), T0p, AF.Relu, bias=64.0, scale=-64.0)]
    rm = act(new("FF"), mm(psum(), terms=[(F1, room), (IZ, nwd[2])]), AF.Copy)
    c0 = ts(new("FF"), siz, 0.5, float(SENT), A.is_lt, A.mult)
    Cf = tt(c0, c0, cur, A.max)
    Cu = cp(new("UU"), Cf)
    Cn = ts(new("FF"), cur, 8192.0 + OFF, None, A.add)
    PPr, GL, LE, EE = reg("PP", 0, M), reg("GL", 0, M), reg("LE", 0, M), reg("EE", 0, M)
    has, hs, sig = new("BB"), new("BB"), new("BB", 256)
    G1, G2 = new("BB", 256), new("HH", 256)

    def part(terms, lo, n):
        return [(l, sub(r, lo, n)) for l, r in terms]

    def choose(t, pen):
        at("M", t)
        sgather(GL, KWIN[t], klu)
        vgather(LE, KWIN[t], kru, GL, A.is_ge)
        emp = act(new("BB"), tolist(psum(), [(R4, GL)]), AF.Relu, bias=-254.0 * 4, scale=4.0)
        ss, tl = new("BB", 256), new("FF", 256)
        sr, sn = sub(ss, 0, 128), sub(ss, 128, 128)
        for lo, n in chunks(128, PAR["DCH"][t]):
            c = lambda r: sub(r, lo, n)
            pl = tolist(psum(n), [(ALL, sub(LE, 16 * lo, 16 * n))], [(I1, c(x)) for x in pen + [emp]])
            ts(c(sr), pl, 8.5, None, A.is_lt)
            ts(c(sn), pl, 16.5, None, A.is_gt)
            if n == 128:
                tt(tl, ss, kh, A.mult)
            else:
                tt(c(tl), c(sr), c(kh), A.mult)
                tt(sub(tl, 128 + lo, n), c(sn), sub(kh, 128 + lo, n), A.mult)
        return sn, [(F1, sub(tl, 0, 128)), (F1, sub(tl, 128, 128))]

    def cast(o, terms, s1, s2=None, ch=128):
        for lo, n in chunks(128, ch):
            ts(sub(o, lo, n), mm(psum(n), terms=part(terms, lo, n)), s1, s2, *((A.add, A.min) if s2 else (A.add,)))
        return o

    def keys(t, terms, s1):
        sgather(K[t + 1], KWIN[t], cast(new("UU"), terms, s1, float(M), PAR["DCH"][t]))

    for t in range(RO):
        ptu = new("UU")
        if t == 0 or not PAR["MERGE"]:
            at("M", t)
            pen = [nwl[0]] if t == 0 else [nwd[t], act(new("BB"), mm(psum(), terms=[(I1, (nwl[1], cond)[t - 1]), (IN, gone)]),
                                                       AF.Relu, scale=64.0)]
            sn, step0 = choose(t, pen)
            owu, of, pf_ = new("UU"), new("FF"), new("FF")
            for lo, n in chunks(128, PAR["DCH"][t]):
                po = mm(psum(n), terms=part([(F1, cV)] + step0, lo, n))
                cp(sub(owu, lo, n), po)
                act(sub(of, lo, n), po, AF.Copy)
            at("K", t)
            mine = [(F1, of), (IZ, sn)]
            keys(t, mine + ([(I1, tt(new("BB"), sn, gone, A.mult))] if t else []), -4096.0)
            at("W", t)
            if t:
                torow("Y", WA, dh, dl)
            scatter("V", W[0], owu, SB, PAR["SCH"])
            for lo, n in chunks(128, 64):
                pq = mm(psum(n), [(R08, sub(WA, 16 * lo, 16 * n))], part(mine + [(F1, cG)], lo, n))
                ts(sub(ptu, lo, n), pq, -4096.0, None, A.add)
                act(sub(pf_, lo, n), pq, AF.Copy)
            gone = act(new("BB"), mm(psum(), terms=[(F1, pf_), (FN, of), (IQ, sn)]), AF.Abs, scale=4096.0)
        elif t == 1:
            at("M", 1)
            pen = act(new("BB"), mm(psum(), terms=[(I1, nwl[1]), (IN, gone)]), AF.Relu, scale=64.0)
            sn, step1 = choose(1, [nwd[1], pen])
            at("K", 1)
            mine = [(F1, cV), (IZ, sn)] + step1
            keys(1, mine + [(I1, tt(new("BB"), sn, gone, A.mult))], -4096.0)
            at("M", 2)
            both = act(new("FF"), mm(psum(), terms=[(F1, cV), (FN, kv), (IK, cond)] + step1), AF.Copy)
            sn2, step2 = choose(2, [nwd[2]])
            at("W", 1)
            owu = cast(new("UU"), [(F1, both)] + step2, 0.0, None, PAR["DCH"][2])
            mine = [(F1, act(new("FF"), mm(psum(), terms=mine), AF.Copy))]
            torow("Y", WA, dh, dl)
            scatter("V", W[1], owu, SB, PAR["SCH"])
            pa0, paf = new("FF"), new("FF")
            for lo, n in chunks(128, 64):
                pa = mm(psum(n), [(R08, sub(WA, 16 * lo, 16 * n))], [(F1, sub(cG, lo, n))])
                tt(sub(pa0, lo, n), pa, sub(par0, lo, n), A.mult)
                act(sub(paf, lo, n), pa, AF.Copy)
            cast(ptu, [(F1, pa0)] + mine, -4096.0, None, 64)
            gone = act(new("BB"), pa0, AF.Abs, scale=4096.0)
        else:
            at("W", 2)
            go = ts(new("BB"), mm(psum(), terms=[(IG, sn2), (IK, cond), (IN, gone)]), 0.5, None, A.is_lt)
            mine = [(F1, vv), (IQ, go), (F1, tt(new("FF"), mm(psum(), terms=[(FN, kv)] + step2), go, A.mult))]
            at("K", 2)
            keys(2, mine + [(I1, gone), (IN, tt(new("BB"), go, gone, A.mult))], 0.0)
            at("W", 2)
            pb = tolist(psum(), [(R08, WB)], [(F1, cG)], ch=128)
            pbf, gb = act(new("FF"), pb, AF.Copy), act(new("BB"), pb, AF.Sign)
            act(gb, gb, AF.Abs)
            ga = act(new("BB"), mm(psum(), terms=[(F1, paf), (FN, pa0)]), AF.Abs, scale=4096.0)
            cast(ptu, [(F1, pbf), (F1, paf), (FN, pa0)] + mine, 0.0)
        at("P", t)
        Q, S2, S3 = reg("QQ", 0, M), reg("SR", 0, M), reg("SR", M, M)
        old = NG[t]
        sgather(PPr, old, Cu)
        hv = act(new("FF"), tolist(psum(), [(R08, PPr)]), AF.Copy)
        if t == 0:
            dma("Y", [ZR], [PPr], [(lambda: rows(PPr, 4, 8), lambda: rows(ZR, 4, 8))], 65536, nrows=16)
        at("Q", t)
        sgather(Q, PPr, ptu)
        su = [new("UU") for _ in range(3)]
        sf = [new("FF") for _ in range(3)]
        D, dab, dk, e = new("FF"), new("FF"), new("BB"), new("BB")
        if t == 2 and PAR["MERGE"]:
            hx = act(new("FF"), mm(psum(), terms=[(FN, hv), (IX, gb), (IX, gb)]), bias=-65536.0, scale=-1.0)
            gone = ga
        for lo, n in chunks(128, 64):
            c = lambda r: sub(r, lo, n)
            if t < 2 or not PAR["MERGE"]:
                p = tolist(psum(n), [(R08, sub(Q, 16 * lo, 16 * n))], [(I1, c(gone))])
                ts(c(su[0]), p, -OFF, float(SENT), A.add, A.min)
                act(c(sf[0]), p, AF.Copy)
                continue
            p = tolist(psum(n), [(R08, sub(Q, 16 * lo, 16 * n))], [(I1, c(ga)), (IX, c(gb))])
            tt(c(sf[0]), p, c(hx), A.max)
            ts(c(su[0]), c(sf[0]), -OFF, float(SENT), A.add, A.min)
        for lo, n in chunks(128, PAR["LCH"][t]):
            c = lambda r: sub(r, lo, n)
            p = mm(psum(n), terms=[(F1, c(hv)), (FN, c(sf[0])), (I1, c(gone))])
            act(c(dab), p, AF.Abs)
            ts(c(dk), c(dab), float(IT), None, A.is_lt)
            tt(c(D), p, c(dk), A.mult)
            act(c(dab), c(D), AF.Abs)
        at("N", t)
        if t == 0:
            fill(sub(NG[1], IT, 16), 32768)
            torow("Y", sub(NG[1], 0, IT), act(nhf, nh, AF.Copy), act(nlf, nl, AF.Copy))
        if t == 1:
            dma("Y", [old], [NG[2]], [(lambda: rows(NG[2], 0, 8), lambda: rows(NG[1], 0, 8))], 262144, nrows=16)
        z2 = act(new("BB"), dab, AF.Relu, bias=131072.0, scale=-131072.0)
        du = tt(new("FF"), mm(psum(), terms=[(IN if t else I1, z2), (F1, Cf)]), tO if t else tN, A.max if t else A.min)
        du = ts(new("UU"), du, M - OFF if t else 0.0, None, A.add)
        dma("G", [Q], [SF], [(lambda: rows(SF, 0, 8), lambda: rows(Q, 0, 8))], 131072, nrows=16)
        if t < 2:
            scatter("S", NS[t], du, SF, PAR["NCH"][t])
        if t == 0:
            at("M", 2)
            pz = tolist(psum(), [(R412, Q)], [(IE, sn)], ch=128)
            cond = tt(new("BB"), act(pz, pz, AF.Relu), rm, A.is_ge)
        at("S", t)
        sgather(S2, old, su[0])
        tmp = new("FF")
        for lo, n in chunks(128, PAR["LCH"][t]):
            c = lambda r: sub(r, lo, n)
            p, q = tolist(psum(n), [(R08, sub(S2, 16 * lo, 16 * n))]), psum(n)
            tt(q, p, c(sf[0]), A.is_equal)
            tt(c(tmp), q, c(D), A.mult)
            tt(c(sf[1]), p, c(tmp), A.add)
            ts(c(su[1]), c(sf[1]), -OFF, float(SENT), A.add, A.min)
        at("T", t)
        sgather(S3, old, su[1])
        for lo, n in chunks(128, PAR["LCH"][t]):
            c = lambda r: sub(r, lo, n)
            p, q = tolist(psum(n), [(R08, sub(S3, 16 * lo, 16 * n))]), psum(n)
            tt(c(e), p, c(hv), A.is_equal)
            tt(q, p, c(sf[0]), A.is_equal)
            tt(q, q, c(e), A.subtract)
            tt(c(tmp), q, c(D), A.mult)
            tt(c(sf[2]), p, c(tmp), A.add)
            ts(c(su[2]), c(sf[2]), -OFF, float(SENT), A.add, A.min)
        if t == 2:
            at("N", t)
            scatter("S", NS[2], du, SF, PAR["NCH"][2])
        Cf, Cu = sf[2], su[2]
        at("C", t)
        if t < 2:
            Cn = act(Cn, tt(Cn, Cn, Cf, A.min), bias=8192.0)
        else:
            ci = tt(new("II"), Cn, Cf, A.min)
            Cn = cp(Cn, ts(ci, ci, 8191, None, A.bitwise_and))
        sg = [sub(sig, 0, 128), sub(sig, 128, 128)]
        for k in range(3):
            at("XYZ"[k], t)
            pc = psum()
            for h in range(2):
                l, u, o = reg("LT", k * M + 1024 * h, 1024), sub(su[k], 64 * h, 64), sub(pc, 64 * h, 64)
                ex = [(I8, sub(x, 64 * h, 64)) for x in (sg if k == 2 else [])]
                if 2 * k + h in PAR["XS"][t]:
                    sgather(l, XG, u)
                    for j in (0, 512):
                        d = mm(psum(512), terms=[(I1, sub(l, j, 512)), (IN, sub(K[t + 1], 1024 * h + j, 512))])
                        act(sub(l, j, 512), d, AF.Sign, bias=-0.5, scale=-1.0)
                    mm(o, [(AH, l)], [(I8, sub(fill(new("BB", 64), 1), 0, 64))] + ex)
                else:
                    vgather(l, XG, u, sub(K[t + 1], 1024 * h, 1024), A.is_lt)
                    mm(o, [(ALL, l)], ex)
            if k < 2:
                act(sg[k], pc, AF.Sign, bias=-8.5)
        at("E", t)
        y3 = act(new("FF"), mm(psum(), terms=[(F1, sf[2]), (IZ, sg[0]), (IZ, sg[1])]), bias=6144.0 - OFF)
        tt(y3, mm(psum(), terms=[(F1, sf[1]), (IZ, sg[0]), (IQ, sg[1]), (I1, C6K)]), y3, A.min)
        tt(sub(T3, 0, 128), mm(psum(), terms=[(F1, sf[0]), (IE, sg[0]), (I1, C6K)]), y3, A.min)
        ts(has, pc, -7.5, None, A.is_gt)
        op("V", vc(128, 0.5), [has], [hs],
           lambda: g.vector.tensor_tensor_scan(ap(hs), ap(has), ap(has), 0.0, A.add, A.max), "scan")
        nve = PAR["NVE"][t]
        cv = mm(psum(8), terms=[(hs, GI)])
        if nve < 8:
            cs = act(new("FF", 8), mm(psum(8), terms=[(hs, GI)]), bias=0.5, scale=-1.0)
        sd, rv = reg("SD", 272 * t, 272), reg("RV", 272 * t, 272)
        nv = ts(sub(sd, 256, 16), sub(vv, 0, 16), mm(psum(1), terms=[(BD, sub(hs, 127, 1))]), 8192.0, A.is_ge, A.mult)
        send(2 * t, nv, sub(rv, 256, 16))
        for j in range(8):
            if j < nve:
                ts(sub(EE, 256 * j, 256), KI, sub(cv, j, 1), 2.0, A.is_ge, A.mult)
            else:
                act(sub(EE, 256 * j, 256), KI, AF.Sign, bias=sub(cs, j, 1))
        tt(sub(T1, 0, 128), mm(psum(), terms=[(BD, hs), (NUP, has)]), has, A.mult)
        pb = psum(16)
        op("P", 0.06 + 1024 * PEC, [EE, ONE], [pb],
           lambda pb=pb: [g.tensor.matmul(ap(sub(pb, b, 1)), T.EE[:, b::16], ap(sub(ONE, 0, 1)), True, True)
                          for b in range(16)][-1], "mm")
        colu = ts(new("UU", 16), pb, offe[nve], 0.5, A.add, A.mult)
        vgather(G1, T1, colu, X1, A.is_equal)
        vgather(G2, T3, colu, G1, A.mult)
        pe = mm(psum(16), [(ALH, G2)])
        sgather(sub(sd, 0, 256), XG, ts(new("UU", 16), pe, 2048.0, None, A.add))
        send(2 * t + 1, sub(sd, 0, 256), sub(rv, 0, 256))
        ef = act(new("FF", 16), pe, bias=2048.0)
        pd = mm(psum(16), terms=[(F1, ef), (I1, nv), (I1, sub(rv, 256, 16))])
        scatter("V", XS_, cp(new("UU", 16), tt(new("FF", 16), pd, tX, A.min)), sub(rv, 0, 256), 256)
    at("O", 0)
    none = act(new("BB"), sf[0], AF.Relu, bias=-2048.0 * (OFF + IT - 1), scale=2048.0)
    sgather(GL, KWIN[3], ts(new("UU"), mm(psum(), terms=[(F1, vv), (I1, none)]), float(M), None, A.min))
    dma("S", [GL], [], [(lambda: T.yk[:], lambda: ap(GL))], 524288)
    dma("S", [Cn], [], [(lambda: T.yc[:], lambda: ap(Cn))], 65536)
    NE = sub(NG[2], 0, IT)
    dma("Y", [NE], [nhf, nlf], [(lambda: ap(nhf), lambda: rows(NE, 0, 16)), (lambda: ap(nlf), lambda: rows(NE, 8, 16))],
        262144, nrows=256)
    ne = cp(nhf, ts(nx, mm(psum(256), terms=[(F1, nhf), (F1, nlf)]), -OFF, None, A.add))
    dma("S", [ne], [], [(lambda: T.yn[:], lambda: ap(ne))], 131072)
    dma("Y", [XS_], [], [(lambda: T.yx[:], lambda: T.XX[:, 0:IT])], 1048576)
    return ops, bank


def depends(ops):
    def clash(a, b):
        return a[1] < b[2] and b[1] < a[2] and (a[3] is None or b[3] is None or a[3] == b[3])

    seen = {}
    for k, o in enumerate(ops):
        dep = set()
        for r in o["rd"]:
            dep.update(j for j, q, w in seen.get(r[0], ()) if w and clash(r, q))
        for r in o["wr"]:
            dep.update(j for j, q, w in seen.get(r[0], ()) if clash(r, q))
        for r in o["rd"]:
            seen.setdefault(r[0], []).append((k, r, False))
        for r in o["wr"]:
            seen.setdefault(r[0], []).append((k, r, True))
        dep.discard(k)
        o["dep"] = sorted(dep)
        o["pv"] = sorted(set(r[0] for r in o["rd"] + o["wr"] if isinstance(r[0], tuple)))


def place(seq, pred, eng, dur, pre, post):
    busy, st, fin = {e: [] for e in eng}, [0.0] * len(dur), [0.0] * len(dur)
    for k in seq:
        s, d = pre[k], dur[k]
        if pred[k]:
            s += max([fin[j] for j in pred[k]])
        if d:
            lst = busy[eng[k]]
            i = n = len(lst)
            while i and lst[i - 1][1] > s:
                i -= 1
            while i < n and s + d > lst[i][0]:
                if lst[i][1] > s:
                    s = lst[i][1]
                i += 1
            lst.insert(i, (s, s + d))
        st[k], fin[k] = s, s + d + post[k]
    return st, fin


def deal(ops, seq, eng):
    left, bank = {}, {}
    for o in ops:
        for v in o["pv"]:
            left[v] = left.get(v, 0) + 1
    holder, last = [None] * 8, [-1] * 8
    pos, dep, order, rest = {}, {}, [], list(seq)
    while rest:
        for i, k in enumerate(rest):
            o = ops[k]
            if all(j in pos for j in o["dep"]) and sum(v not in bank for v in o["pv"]) <= holder.count(None):
                break
        else:
            return None
        del rest[i]
        d = set(o["dep"])
        for v in o["pv"]:
            fresh = v not in bank
            if fresh:
                bank[v] = min((pos.get(last[b], -1), b) for b in range(8) if holder[b] is None)[1]
                holder[bank[v]] = v
            b = bank[v]
            if last[b] >= 0 and (fresh or eng[last[b]] != eng[k]):
                d.add(last[b])
            last[b] = k
        for v in o["pv"]:
            left[v] -= 1
            if left[v] == 0:
                holder[bank[v]] = None
        pos[k] = len(order)
        order.append(k)
        dep[k] = d
    return order, bank, dep


def costs(ops, m):
    gather, scatter, tensor, other, fixed, wake, dma, remote = m
    dur, lat = [], []
    for o in ops:
        d, f, name = o["dur"], 0.06, o["name"]
        if o["kind"] == "c":
            r = {"sg": gather, "vg": gather, "sc": scatter, "mm": tensor}.get(name, other)
            d = (d - f) * r + (f if name in ("sg", "vg", "sc", "iota") else f * fixed)
        dur.append(d * remote / 2.5 if o["eng"] == "G" and o["kind"] != "c" else d)
        lat.append({"c": wake, "m": o["lat"] + dma, "d": 0.0, "r": 0.0}.get(o["kind"], remote - 0.4))
    return dur, lat


COSTS = ((0.72, 0.6, 1.25, 1.15, 0.6, 0.15, 1.6, 3.2), (1.45, 1.8, 1.15, 1.15, 0.5, 0.1, 1.5, 2.5),
         (0.75, 1.3, 0.9, 0.9, 0.7, 0.15, 2.0, 3.0), (1.2, 0.6, 1.2, 1.1, 0.5, 0.12, 1.4, 2.6),
         (0.88, 0.88, 1.0, 1.0, 0.6, 0.14, 1.5, 2.8))
WEIGHT = (80.0, 160.0, 120.0, 115.0, 60.0)


def schedule(ops):
    n = len(ops)
    pred, succ = [o["dep"] for o in ops], [[] for _ in ops]
    for k in range(n):
        for j in pred[k]:
            succ[j].append(k)
    eng, dur, lat, zero = [o["eng"] for o in ops], [o["dur"] for o in ops], [o["lat"] for o in ops], [0.0] * n
    anc, near = [0] * n, []
    for k in range(n):
        far = 0
        for j in pred[k]:
            far |= anc[j]
        near.append([j for j in pred[k] if not far >> j & 1])
        anc[k] = far | sum(1 << j for j in pred[k])
    steps = [o["step"] for o in ops]
    after = [[] for _ in ops]
    for k in range(n):
        for j in near[k]:
            after[j].append(k)

    either = ["alt" in o for o in ops]

    def first(due, shift=zero):
        key, eng = [0.0] * n, [o["eng"] for o in ops]
        for k in reversed(range(n)):
            key[k] = min([due[steps[k]]] + [key[j] for j in after[k]]) - dur[k] - lat[k] + shift[k]
        wait, ready, free, order = [len(p) for p in near], [0.0] * n, {e: 0.0 for e in eng}, []
        left, bank, idle, last = dict(uses), {}, list(range(8)), [0.0] * 8
        can = [k for k in range(n) if not wait[k]]
        while can:
            low, cand = 1e9, []
            for k in can:
                s = max(ready[k], free[eng[k]])
                need = 0
                for v in pvs[k]:
                    if v in bank:
                        s = max(s, last[bank[v]])
                    else:
                        need += 1
                if need:
                    if need + spare[k] > len(idle):
                        continue
                    s = max(s, last[idle[0]])
                cand.append((key[k], k, s, eng[k]))
                if s + dur[k] < low:
                    low, e = s + dur[k], eng[k]
                if either[k]:
                    s2 = max(ready[k], free["V"])
                    if s2 < s - due["gap"]:
                        cand.append((key[k] + due["bias"], k, s2, "V"))
                        if s2 + dur[k] < low:
                            low, e = s2 + dur[k], "V"
            if not cand:
                return None
            cand = [c for c in cand if c[3] == e]
            soon = min(c[2] for c in cand)
            soon += PAR["LOOK"] * (low - soon)
            k, s = min(c for c in cand if c[2] <= soon)[1:3]
            eng[k] = e
            can.remove(k)
            order.append(k)
            if e:
                free[e] = s + dur[k]
            f = s + dur[k] + lat[k]
            for v in pvs[k]:
                if v not in bank:
                    bank[v] = idle.pop(0)
                last[bank[v]] = f
                left[v] -= 1
                if not left[v]:
                    idle.append(bank[v])
            for j in after[k]:
                ready[j] = max(ready[j], f)
                wait[j] -= 1
                if not wait[j]:
                    can.append(j)
        return order, eng

    durs, lats = zip(*[costs(ops, m) for m in COSTS])
    dur, lat = durs[-1], lats[-1]
    pvs = [o["pv"] for o in ops]
    uses = {}
    for p in pvs:
        for v in p:
            uses[v] = uses.get(v, 0) + 1
    spare = [1 if len(p) == 1 else 0 for p in pvs]

    marks = [max(k for k in range(n) if steps[k] == s) for s in PAR["MARK"].split()]
    timed = [[k - 1] if ops[k]["kind"] == "m" else near[k] for k in range(n)]

    def judge(order, eng, same=0, old=None):
        left, bank, free, last, dep, qp, at = dict(uses), {}, list(range(8)), [-1] * 8, list(timed), [-1] * n, {}
        for k in order:
            e = eng[k]
            if e:
                qp[k] = at.get(e, -1)
                at[e] = k
            for v in pvs[k]:
                b = bank.get(v)
                if b is None:
                    if not free:
                        return None
                    b = bank[v] = free.pop(0)
                    if last[b] >= 0:
                        dep[k] = dep[k] + [last[b]]
                elif eng[last[b]] != e:
                    dep[k] = dep[k] + [last[b]]
                last[b] = k
            for v in pvs[k]:
                left[v] -= 1
                if not left[v]:
                    free.append(bank[v])
        sc, out, rest = 0.0, [], order[same:]
        for m, (du, la, w) in enumerate(zip(durs, lats, WEIGHT)):
            fin, end = (list(old[m][0]), list(old[m][1])) if same else ([0.0] * n, [0.0] * (n + 1))
            for k in rest:
                s = end[qp[k]]
                for j in dep[k]:
                    if fin[j] > s:
                        s = fin[j]
                s += du[k]
                end[k] = s
                fin[k] = s + la[k]
            sc += (max(fin) + PAR["PULL"] * sum(fin[k] for k in marks)) / w
            out.append((fin, end))
        return sc, out, dep, qp, bank

    rng = np.random.RandomState(PAR["SEED"])
    due = dict(PAR["DUE"])
    names = sorted(due)
    order, eng = first(due)
    now = judge(order, eng)
    for it in range(PAR["ROUGH"]):
        d2 = dict(due)
        for _ in range(rng.randint(1, 3)):
            x = names[rng.randint(len(names))]
            d2[x] += float(rng.randn()) * (0.5 if x == "gap" else 3.0)
        o2 = first(d2)
        got = o2 and judge(*o2)
        if got and got[0] < now[0] + PAR["MIDT"] * (1.0 - it / PAR["ROUGH"]) * rng.rand():
            now, order, eng, due = got, o2[0], o2[1], d2
    FOUND_DUE.append(due)

    def critical(now, m):
        (fin, end), dep, qp = now[1][m], now[2], now[3]
        k, arcs, flex = marks[rng.randint(len(marks))] if rng.rand() < 0.4 else fin.index(max(fin)), [], []
        while k >= 0:
            s, j = end[k] - durs[m][k], -1
            for i in dep[k]:
                if fin[i] > s - 1e-9:
                    j = i
            if j < 0 and qp[k] >= 0 and end[qp[k]] > s - 1e-9:
                j = qp[k]
            if j >= 0 and not anc[k] >> j & 1:
                arcs.append((j, k))
            if "alt" in ops[k]:
                flex.append(k)
            k = j
        return arcs, flex

    best, tries = (now[0], order, eng), PAR["TRIES"]
    for it in range(tries):
        arcs, flex = critical(now, rng.randint(len(COSTS)))
        qp = now[3]
        o2, e2 = order, eng
        if flex and rng.rand() < PAR["FLIP"][1]:
            k = flex[rng.randint(len(flex))]
            e2 = list(eng)
            e2[k] = "V" if e2[k] == "S" else "S"
            a = order.index(k)
        elif not arcs:
            continue
        else:
            j, k = arcs[rng.randint(len(arcs))]
            ahead = rng.rand() < 0.5
            while ahead and rng.rand() < 0.5 and qp[j] >= 0 and not anc[k] >> qp[j] & 1:
                j = qp[j]
            a, b = order.index(j), order.index(k) + 1
            if not ahead:
                b = min(n, b + rng.randint(0, 2) * rng.randint(0, 30))
            seg = order[a:b]
            if ahead:
                front = [x for x in seg if x == k or anc[k] >> x & 1]
                back = [x for x in seg if not (x == k or anc[k] >> x & 1)]
            else:
                front = [x for x in seg if not (x == j or anc[x] >> j & 1)]
                back = [x for x in seg if x == j or anc[x] >> j & 1]
            o2 = order[:a] + front + back + order[b:]
        got = judge(o2, e2, a, now[1])
        if got and (got[0] < now[0] or rng.rand() < np.exp((now[0] - got[0]) / (PAR["TEMP"] * (1.0 - it / tries) + 1e-4))):
            now, order, eng = got, o2, e2
            if now[0] < best[0]:
                best = (now[0], order, eng)
    got = judge(best[1], best[2])
    dep = {k: set(pred[k]) | set(got[2][k]) for k in range(n)}
    return best[0], (best[1], got[4], dep, best[2]), [max(f) for f, e in got[1]]


FOUND = []
FOUND_DUE = []


def rank_program(g, core, T, topo):
    rank = T.rank_of(core)
    if rank is None:
        return
    n = len(T.cores)
    nxt, prv = T.cores[(rank + 1) % n], T.cores[(rank - 1) % n]
    assert topo.may_write(core, nxt)
    rid, pid, _ = topo.addr(nxt)
    n_out, n_in = len(topo.engines(core, nxt)), len(topo.engines(prv, core))
    ops, bank = plan(T, g, (rid, pid, topo.mask(core, nxt)))
    depends(ops)
    if not FOUND:
        FOUND.append(schedule(ops)[1])
    order, banks, dep, eng = FOUND[0]
    for o, e in zip(ops, eng):
        if e != o["eng"]:
            o.update(eng=e, fn=o["alt"])
    bank.update(banks)
    pos = {k: i for i, k in enumerate(order)}
    queue = {"V": g.vector, "S": g.scalar, "P": g.tensor, "G": g, "Y": g.sync}
    known = {q: {} for q in queue}
    count = {"V": 0, "S": 0, "P": 0, "G": 0}
    nd, final = 0, {}
    for k in order:
        o = ops[k]
        if o["name"] == "recv":
            o["tok"], o["clock"] = (o["kind"], n_in), {}
            final[o["kind"]] = n_in
            continue
        if o["kind"] == "m":
            o["tok"], o["clock"] = ops[k - 1]["tok"], ops[k - 1]["clock"]
            continue
        kn = known[o["eng"]]
        for j in sorted(dep[k], key=lambda j: -pos[j]):
            if ops[j]["kind"] == "d":
                continue
            s, v = ops[j]["tok"]
            if kn.get(s, 0) < v:
                queue[o["eng"]].wait_ge(T.sem[s], v)
                kn[s] = v
                for s2, v2 in ops[j]["clock"].items():
                    kn[s2] = max(kn.get(s2, 0), v2)
        o["clock"] = dict(kn)
        r = o["fn"]()
        if o["kind"] == "c":
            count[o["eng"]] += 1
            o["tok"] = ("c" + o["eng"], count[o["eng"]])
            r.then_inc(T.sem[o["tok"][0]], 1)
        elif o["kind"] == "d":
            o["tok"] = ("d%d" % nd, o["inc"])
            nd += 1
            for x in r:
                x.then_inc(T.sem[o["tok"][0]], 16)
        else:
            continue
        final[o["tok"][0]] = o["tok"][1]
    for t in range(2 * RO):
        final["sn%d" % t] = n_out
    for s, v in final.items():
        g.sync.wait_ge(T.sem[s], v)
